import numpy as np
import ml_dtypes


def mxq(x, axis, fmt="e4m3"):
    dtype, down = {"e4m3": (ml_dtypes.float8_e4m3fn, 7), "e5m2": (ml_dtypes.float8_e5m2, 14)}[fmt]
    v = np.moveaxis(np.asarray(x, np.float32).astype(ml_dtypes.bfloat16).astype(np.float64), axis, -1)
    blocks = v.reshape(v.shape[:-1] + (-1, 32))
    amax = np.abs(blocks).max(-1, keepdims=True)
    byte = np.maximum(np.where(amax > 0, np.frexp(amax)[1] - 1 + 127, 0) - down, 1)
    scale = np.exp2(byte - 127.0)
    codes = (blocks / scale).astype(np.float32).astype(dtype).astype(np.float64)
    return np.moveaxis((codes * scale).reshape(v.shape), -1, axis)


WIDE = False


def mx_kscale(k):
    if not WIDE:
        return np.ones(k)
    levels = np.array([10, -10, 5, -5, 0])
    if k % 512:
        return np.exp2(np.random.permutation(np.resize(levels, k // 32))).repeat(32)
    a = np.empty((k // 512, 16))
    for p in range(k // 512):
        a[p, :8] = np.random.permutation(np.resize(levels, 8))
        for g in range(8):
            far = levels[np.abs(levels - a[p, g]) >= 10]
            a[p, g + 8] = far[np.random.randint(len(far))]
    return np.exp2(a.ravel()).repeat(32)


def f64(x):
    return np.asarray(x).astype(np.float64)


def striped(idx):
    return np.tile(idx.reshape(-1, 16).T, (8, 1)).astype(np.uint16)


def unstriped(offs):
    return offs[:16].T.reshape(-1).astype(np.int64)


def pack_weight(w):
    k, n = w.shape
    w = f64(np.asarray(w, np.float32).astype(ml_dtypes.bfloat16)).reshape(k // 32, 32, n)
    amax = np.abs(w).max(1)
    byte = np.clip(np.where(amax > 0, np.frexp(amax)[1] - 1 + 127 - 7, 1), 1, 254)
    scaled = (w * np.exp2(127.0 - byte)[:, None, :]).reshape(k, n).astype(np.float32)
    words = np.ascontiguousarray(scaled.reshape(k // 512, 128, 4, n).transpose(0, 1, 3, 2)).astype(ml_dtypes.float8_e4m3fn).view(np.uint8)
    return words, np.ascontiguousarray(byte.astype(np.uint8).reshape(k // 512, 16, n))


def unpack_weight(words, scales):
    g, p, n, _ = words.shape
    vals = np.ascontiguousarray(words).view(ml_dtypes.float8_e4m3fn).astype(np.float64) * np.repeat(np.exp2(scales.astype(np.float64) - 127.0), 8, axis=1)[..., None]
    return vals.transpose(0, 1, 3, 2).reshape(g * 512, n)


def planes(y):
    n, m = y.shape
    v = y.astype(np.float32).astype(ml_dtypes.bfloat16).astype(np.float64).reshape(n // 32, 32, m)
    top = np.abs(v).max(1)
    byte = np.clip(np.where(top > 0, np.frexp(top)[1] - 1 + 127 - 7, 1), 1, 254)
    codes = (v * np.exp2(127.0 - byte)[:, None, :]).reshape(n, m).astype(np.float32).astype(ml_dtypes.float8_e4m3fn).view(np.uint8)
    words = codes.reshape(n // 512, 128, 4, m).transpose(0, 1, 3, 2)
    return np.ascontiguousarray(words), np.ascontiguousarray(byte.astype(np.uint8).reshape(n // 512, 16, m))


K, T, S, V, H, N, W = 512, 1024, 512, 256, 512, 512, 1024


def setup_inputs():
    n = np.random.standard_normal
    s = mx_kscale(K)[:, None]
    u = mx_kscale(H)
    near = np.random.permutation(S)
    far = np.random.permutation(S)
    packed_xT = pack_weight(n((K, T)) * s)
    packed_eT = pack_weight(n((K, W)) * s)
    packed_w2 = pack_weight(n((K, N)) / np.sqrt(K) / s)
    packed_w3 = pack_weight(n((H, N)) / np.sqrt(H) / u[:, None])
    return {
        "x_words": packed_xT[0],
        "x_scales": packed_xT[1],
        "e_words": packed_eT[0],
        "e_scales": packed_eT[1],
        "w1": (n((K, H)) / np.sqrt(K) / s * u).astype(np.float32),
        "w2_words": packed_w2[0],
        "w2_scales": packed_w2[1],
        "w3_words": packed_w3[0],
        "w3_scales": packed_w3[1],
        "offs": striped(np.random.permutation(T)[:S]),
        "pos1": striped(near[:V]),
        "pos2": striped(near[V:]),
        "attr": striped(np.random.permutation(W)[:S]),
        "edge1": striped(far[:V]),
        "edge2": striped(far[V:]),
    }


def reference(x_words, x_scales, e_words, e_scales, w1, w2_words, w2_scales, w3_words, w3_scales, offs, pos1, pos2, attr, edge1, edge2):
    e_attr = unpack_weight(e_words, e_scales)[:, unstriped(attr)]
    r = unpack_weight(w2_words, w2_scales).T @ e_attr
    r0 = r[:, unstriped(edge1)]
    xq = unpack_weight(x_words, x_scales)[:, unstriped(offs)]
    h = mxq(f64(w1), 0, "e4m3").T @ xq
    r1 = r[:, unstriped(edge2)]
    z = r0 * h[:, unstriped(pos1)] + r1 * h[:, unstriped(pos2)]
    out_0 = unpack_weight(w3_words, w3_scales).T @ mxq(z, 0, "e4m3")
    return (out_0,) + planes(out_0)

@@ -1,0 +1,224 @@
+from contextlib import ExitStack
+
+import concourse.mybir as mybir
+
+F32 = mybir.dt.float32
+BF16 = mybir.dt.bfloat16
+I32 = mybir.dt.int32
+U32 = mybir.dt.uint32
+U16 = mybir.dt.uint16
+U8 = mybir.dt.uint8
+FP8X4 = mybir.dt.float8_e4m3fn_x4
+MULT = mybir.AluOpType.mult
+ADD = mybir.AluOpType.add
+
+P = 128
+PACK = 4
+TABLE = 1024
+PICKED = 512
+TARGETS = 256
+HALF = 128
+FLOPS = 2 * 512 * 512 * (2 * PICKED + TARGETS)
+
+
+def tile_picked_zcomp_mul_po_kernel(
+    tc, x_words, x_scales, e_words, e_scales, w1, w2_words, w2_scales, w3_words, w3_scales,
+    offs, pos1, pos2, attr, edge1, edge2, out_0, out_1, out_2,
+):
+    nc = tc.nc
+    with ExitStack() as ctx:
+        pool = ctx.enter_context(tc.tile_pool(name="sbuf", bufs=1))
+        psum = ctx.enter_context(tc.psum_pool(name="psum", bufs=1))
+
+        def sb(name, shape, dtype):
+            return pool.tile(shape, dtype, name=name, align_bytes=64)
+
+        def load_list(name, src):
+            tile = pool.tile(list(src.shape), U16, name=name)
+            nc.sync.dma_start(tile[:], src)
+            return tile
+
+        def load_words(name, src):
+            tile = sb(name, [P, src.shape[2]], I32)
+            nc.sync.dma_start(tile[:], src[0].rearrange("p n t -> p (n t)").bitcast(I32))
+            return tile
+
+        def cleared_plane(name, width):
+            tile = sb(name, [P, width], U8)
+            nc.vector.memset(tile[:].bitcast(I32), 0)
+            return tile
+
+        def load_scales(tile, src, queue):
+            for q in range(4):
+                queue.dma_start(tile[32 * q : 32 * q + 4, :].bitcast(I32), src[0, 4 * q : 4 * q + 4, :].bitcast(I32))
+
+        def deal(name, words, scales):
+            dealt_words = sb(name + "_words_dealt", [P, 512], I32)
+            dealt_scales = sb(name + "_scales_dealt", [P, 512], U8)
+            nc.vector.tensor_copy(
+                dealt_words[:].rearrange("p (t c i) -> p c t i", t=PACK, i=4),
+                words[:].rearrange("p (c i t) -> p c t i", t=PACK, i=4),
+            )
+            nc.vector.tensor_copy(
+                dealt_scales[:].rearrange("p (t m) -> p m t", t=PACK),
+                scales[:].rearrange("p (m t) -> p m t", t=PACK),
+            )
+            return dealt_words, dealt_scales
+
+        def gather_words(name, words, offsets):
+            picked = sb(name, [P, PICKED], U32)
+            nc.vector.tensor_copy(picked[:], words[:].bitcast(U32).indirect(offsets[:]))
+            return picked
+
+        def gather_scales(name, scales, offsets):
+            picked = sb(name, [P, PICKED], U8)
+            nc.vector.tensor_copy(picked[:], scales[:].indirect(offsets[:]))
+            return picked
+
+        def project(name, w_words, w_scales, words, scales):
+            rows = []
+            for t in range(PACK):
+                cols = slice(t * P, (t + 1) * P)
+                bank = psum.tile([P, PICKED], F32, name="bank", tag="bank", bufs=6)
+                nc.tensor.matmul_mx(
+                    out=bank[:], lhsT=w_words[:, cols].bitcast(FP8X4), lhsT_scale=w_scales[:, cols],
+                    rhs=words[:].bitcast(FP8X4), rhs_scale=scales[:], start=True, stop=True,
+                )
+                row = sb(name + str(t), [P, PICKED], F32)
+                nc.scalar.copy(row[:], bank[:])
+                rows.append(row)
+            return rows
+
+        e_plane = cleared_plane("e_plane", TABLE)
+        w2_plane = cleared_plane("w2_plane", 512)
+        x_plane = cleared_plane("x_plane", TABLE)
+        w3_plane = cleared_plane("w3_plane", 512)
+
+        attr_sb = load_list("attr_sb", attr)
+        e_table = load_words("e_table", e_words)
+        load_scales(e_plane, e_scales, nc.scalar)
+        w2_raw = load_words("w2_raw", w2_words)
+        offs_sb = load_list("offs_sb", offs)
+        x_table = load_words("x_table", x_words)
+        load_scales(w2_plane, w2_scales, nc.scalar)
+        w1_rows = w1.rearrange("(p j) c -> p j c", j=PACK)
+        w1_raw = []
+        for u in range(2):
+            part = sb("w1_raw" + str(u), [P, PACK, 256], F32)
+            nc.sync.dma_start(part[:], w1_rows[:, :, 256 * u : 256 * (u + 1)])
+            w1_raw.append(part)
+            if u == 0:
+                load_scales(x_plane, x_scales, nc.scalar)
+        edges = [load_list("edge1_sb", edge1), load_list("edge2_sb", edge2)]
+        places = [load_list("pos1_sb", pos1), load_list("pos2_sb", pos2)]
+        w3_raw = load_words("w3_raw", w3_words)
+        load_scales(w3_plane, w3_scales, nc.sync)
+
+        e_picked = gather_words("e_picked", e_table, attr_sb)
+        e_picked_scales = gather_scales("e_picked_scales", e_plane, attr_sb)
+        w2_dealt, w2_dealt_scales = deal("w2", w2_raw, w2_plane)
+
+        w1_bf = sb("w1_bf", [P, PACK, P, PACK], BF16)
+
+        def round_w1(u):
+            nc.scalar.copy(
+                w1_bf[:, :, 64 * u : 64 * (u + 1), :].rearrange("p t m j -> p m t j"),
+                w1_raw[u][:].rearrange("p j (m t) -> p m t j", t=PACK),
+            )
+
+        round_w1(0)
+        r_rows = project("r", w2_dealt, w2_dealt_scales, e_picked, e_picked_scales)
+        round_w1(1)
+
+        x_picked = gather_words("x_picked", x_table, offs_sb)
+        x_picked_scales = gather_scales("x_picked_scales", x_plane, offs_sb)
+
+        r_edge = [[None, None] for t in range(PACK)]
+
+        def gather_edges(t):
+            for d in range(2):
+                picked = sb("r_edge%d_%d" % (t, d), [P, TARGETS], F32)
+                nc.vector.tensor_copy(picked[:], r_rows[t][:].indirect(edges[d][:]))
+                r_edge[t][d] = picked
+
+        gather_edges(0)
+        gather_edges(1)
+        w1_words = sb("w1_words", [P, 512], U32)
+        w1_scales = sb("w1_scales", [P, 512], U8)
+        nc.vector.quantize_mx(
+            out=w1_words[:].bitcast(FP8X4), scales=w1_scales[:], in_=w1_bf[:].rearrange("p t m j -> p (t m j)")
+        )
+        h_rows = project("h", w1_words, w1_scales, x_picked, x_picked_scales)
+        gather_edges(2)
+        gather_edges(3)
+        w3_dealt, w3_dealt_scales = deal("w3", w3_raw, w3_plane)
+
+        messages = [[sb("message%d_%d" % (u, d), [P, PACK, HALF], F32) for d in range(2)] for u in range(2)]
+
+        def multiply(u, t):
+            for d in range(2):
+                nc.vector.tensor_tensor(
+                    messages[u][d][:, t, :],
+                    h_rows[t][:].indirect(places[d][:, 8 * u : 8 * (u + 1)]),
+                    r_edge[t][d][:, HALF * u : HALF * (u + 1)],
+                    MULT,
+                )
+
+        z_bf = [sb("z_bf" + str(u), [P, HALF * PACK], BF16) for u in range(2)]
+        z_words = [sb("z_words" + str(u), [P, HALF], U32) for u in range(2)]
+        z_scales = [sb("z_scales" + str(u), [P, HALF], U8) for u in range(2)]
+        y_bank = [psum.tile([P, PACK, HALF], F32, name="y_bank" + str(u)) for u in range(2)]
+        y_f32 = [sb("y_f32" + str(u), [P, PACK, HALF], F32) for u in range(2)]
+        y_bf = [sb("y_bf" + str(u), [P, HALF, PACK], BF16) for u in range(2)]
+        y_words = [sb("y_words" + str(u), [P, HALF], I32) for u in range(2)]
+        y_scales = sb("y_scales", [P, TARGETS], U8)
+        out_rows = out_0.rearrange("(p t) v -> p t v", t=PACK)
+        out_words = out_1[0].rearrange("p v t -> p (v t)").bitcast(I32)
+
+        def add_messages(u):
+            nc.vector.tensor_tensor(
+                z_bf[u][:].rearrange("p (c i t) -> p c t i", t=PACK, i=4),
+                messages[u][0][:].rearrange("p t (c i) -> p c t i", i=4),
+                messages[u][1][:].rearrange("p t (c i) -> p c t i", i=4),
+                ADD,
+            )
+
+        def last_product(u):
+            nc.vector.quantize_mx(out=z_words[u][:].bitcast(FP8X4), scales=z_scales[u][:], in_=z_bf[u][:])
+            for t in range(PACK):
+                cols = slice(t * P, (t + 1) * P)
+                nc.tensor.matmul_mx(
+                    out=y_bank[u][:, t, :], lhsT=w3_dealt[:, cols].bitcast(FP8X4), lhsT_scale=w3_dealt_scales[:, cols],
+                    rhs=z_words[u][:].bitcast(FP8X4), rhs_scale=z_scales[u][:], start=True, stop=True,
+                )
+
+        def store_f32(u):
+            nc.scalar.copy(y_f32[u][:], y_bank[u][:])
+            nc.scalar.dma_start(out_rows[:, :, HALF * u : HALF * (u + 1)], y_f32[u][:])
+
+        def quantize_result(u):
+            cols = slice(HALF * u, HALF * (u + 1))
+            nc.vector.quantize_mx(
+                out=y_words[u][:].bitcast(FP8X4), scales=y_scales[:, cols], in_=y_bf[u][:].rearrange("p v t -> p (v t)")
+            )
+            nc.sync.dma_start(out_words[:, cols], y_words[u][:])
+
+        for t in range(PACK):
+            multiply(0, t)
+        multiply(1, 0)
+        add_messages(0)
+        multiply(1, 1)
+        last_product(0)
+        nc.scalar.copy(y_bf[0][:], y_bank[0][:].rearrange("p t v -> p v t"))
+        store_f32(0)
+        multiply(1, 2)
+        multiply(1, 3)
+        add_messages(1)
+        quantize_result(0)
+        last_product(1)
+        nc.vector.tensor_copy(y_bf[1][:], y_bank[1][:].rearrange("p t v -> p v t"))
+        store_f32(1)
+        quantize_result(1)
+        for q in range(4):
+            queue = nc.sync if q % 2 else nc.scalar
+            queue.dma_start(out_2[0, 4 * q : 4 * q + 4, :].bitcast(I32), y_scales[32 * q : 32 * q + 4, :].bitcast(I32))

@@ -52,18 +52,20 @@ def tile_picked_zcomp_mul_po_kernel(
             for q in range(4):
                 queue.dma_start(tile[32 * q : 32 * q + 4, :].bitcast(I32), src[0, 4 * q : 4 * q + 4, :].bitcast(I32))
 
-        def deal(name, words, scales):
-            dealt_words = sb(name + "_words_dealt", [P, 512], I32)
-            dealt_scales = sb(name + "_scales_dealt", [P, 512], U8)
+        def deal_words(name, words):
+            dealt = sb(name, [P, 512], I32)
             nc.vector.tensor_copy(
-                dealt_words[:].rearrange("p (t c i) -> p c t i", t=PACK, i=4),
+                dealt[:].rearrange("p (t c i) -> p c t i", t=PACK, i=4),
                 words[:].rearrange("p (c i t) -> p c t i", t=PACK, i=4),
             )
+            return dealt
+
+        def deal_scales(name, scales):
+            dealt = sb(name, [P, 512], U8)
             nc.vector.tensor_copy(
-                dealt_scales[:].rearrange("p (t m) -> p m t", t=PACK),
-                scales[:].rearrange("p (m t) -> p m t", t=PACK),
+                dealt[:].rearrange("p (t m) -> p m t", t=PACK), scales[:].rearrange("p (m t) -> p m t", t=PACK)
             )
-            return dealt_words, dealt_scales
+            return dealt
 
         def gather_words(name, words, offsets):
             picked = sb(name, [P, PICKED], U32)
@@ -75,32 +77,29 @@ def tile_picked_zcomp_mul_po_kernel(
             nc.vector.tensor_copy(picked[:], scales[:].indirect(offsets[:]))
             return picked
 
-        def project(name, w_words, w_scales, words, scales):
-            rows = []
-            for t in range(PACK):
-                cols = slice(t * P, (t + 1) * P)
-                bank = psum.tile([P, PICKED], F32, name="bank", tag="bank", bufs=6)
-                nc.tensor.matmul_mx(
-                    out=bank[:], lhsT=w_words[:, cols].bitcast(FP8X4), lhsT_scale=w_scales[:, cols],
-                    rhs=words[:].bitcast(FP8X4), rhs_scale=scales[:], start=True, stop=True,
-                )
-                row = sb(name + str(t), [P, PICKED], F32)
-                nc.scalar.copy(row[:], bank[:])
-                rows.append(row)
-            return rows
+        def project(name, t, w_words, w_scales, words, scales):
+            cols = slice(t * P, (t + 1) * P)
+            bank = psum.tile([P, PICKED], F32, name="bank", tag="bank", bufs=5)
+            nc.tensor.matmul_mx(
+                out=bank[:], lhsT=w_words[:, cols].bitcast(FP8X4), lhsT_scale=w_scales[:, cols],
+                rhs=words[:].bitcast(FP8X4), rhs_scale=scales[:], start=True, stop=True,
+            )
+            row = pool.tile([P, PICKED], F32, name=name + str(t), tag=name + str(t), align_bytes=64)
+            nc.scalar.copy(row[:], bank[:])
+            return row
 
         e_plane = cleared_plane("e_plane", TABLE)
         w2_plane = cleared_plane("w2_plane", 512)
         x_plane = cleared_plane("x_plane", TABLE)
         w3_plane = cleared_plane("w3_plane", 512)
 
-        attr_sb = load_list("attr_sb", attr)
-        e_table = load_words("e_table", e_words)
-        load_scales(e_plane, e_scales, nc.scalar)
         w2_raw = load_words("w2_raw", w2_words)
+        attr_sb = load_list("attr_sb", attr)
+        load_scales(e_plane, e_scales, nc.sync)
+        e_table = load_words("e_table", e_words)
+        load_scales(w2_plane, w2_scales, nc.sync)
         offs_sb = load_list("offs_sb", offs)
         x_table = load_words("x_table", x_words)
-        load_scales(w2_plane, w2_scales, nc.scalar)
         w1_rows = w1.rearrange("(p j) c -> p j c", j=PACK)
         w1_raw = []
         for u in range(2):
@@ -108,100 +107,130 @@ def tile_picked_zcomp_mul_po_kernel(
             nc.sync.dma_start(part[:], w1_rows[:, :, 256 * u : 256 * (u + 1)])
             w1_raw.append(part)
             if u == 0:
-                load_scales(x_plane, x_scales, nc.scalar)
-        edges = [load_list("edge1_sb", edge1), load_list("edge2_sb", edge2)]
+                load_scales(x_plane, x_scales, nc.sync)
+                edges = [load_list("edge1_sb", edge1), load_list("edge2_sb", edge2)]
         places = [load_list("pos1_sb", pos1), load_list("pos2_sb", pos2)]
         w3_raw = load_words("w3_raw", w3_words)
         load_scales(w3_plane, w3_scales, nc.sync)
 
-        e_picked = gather_words("e_picked", e_table, attr_sb)
+        w2_dealt = deal_words("w2_dealt", w2_raw)
         e_picked_scales = gather_scales("e_picked_scales", e_plane, attr_sb)
-        w2_dealt, w2_dealt_scales = deal("w2", w2_raw, w2_plane)
+        e_picked = gather_words("e_picked", e_table, attr_sb)
+        w2_dealt_scales = deal_scales("w2_dealt_scales", w2_plane)
 
-        w1_bf = sb("w1_bf", [P, PACK, P, PACK], BF16)
+        w1_bf = pool.tile([P, PACK, P, PACK], BF16, name="w1_bf", tag="reused", align_bytes=64)
 
-        def round_w1(u):
+        def round_w1(s):
             nc.scalar.copy(
-                w1_bf[:, :, 64 * u : 64 * (u + 1), :].rearrange("p t m j -> p m t j"),
-                w1_raw[u][:].rearrange("p j (m t) -> p m t j", t=PACK),
+                w1_bf[:, :, 32 * s : 32 * (s + 1), :].rearrange("p t m j -> p m t j"),
+                w1_raw[s // 2][:, :, 128 * (s % 2) : 128 * (s % 2 + 1)].rearrange("p j (m t) -> p m t j", t=PACK),
             )
 
         round_w1(0)
-        r_rows = project("r", w2_dealt, w2_dealt_scales, e_picked, e_picked_scales)
         round_w1(1)
+        r_rows = []
+        for t in range(PACK):
+            r_rows.append(project("r", t, w2_dealt, w2_dealt_scales, e_picked, e_picked_scales))
+            if t < 2:
+                round_w1(2 + t)
 
         x_picked = gather_words("x_picked", x_table, offs_sb)
         x_picked_scales = gather_scales("x_picked_scales", x_plane, offs_sb)
 
-        r_edge = [[None, None] for t in range(PACK)]
+        r_edge = []
 
-        def gather_edges(t):
+        def gather_edges(t, rooms):
             for d in range(2):
-                picked = sb("r_edge%d_%d" % (t, d), [P, TARGETS], F32)
-                nc.vector.tensor_copy(picked[:], r_rows[t][:].indirect(edges[d][:]))
-                r_edge[t][d] = picked
+                nc.vector.tensor_copy(rooms[d], r_rows[t][:].indirect(edges[d][:]))
+            r_edge.append(rooms)
 
-        gather_edges(0)
-        gather_edges(1)
-        w1_words = sb("w1_words", [P, 512], U32)
+        for t in range(2):
+            gather_edges(t, [sb("r_edge%d_%d" % (t, d), [P, TARGETS], F32)[:] for d in range(2)])
+        w1_words = pool.tile([P, 512], U32, name="w1_words", tag="r0", align_bytes=64)
         w1_scales = sb("w1_scales", [P, 512], U8)
         nc.vector.quantize_mx(
             out=w1_words[:].bitcast(FP8X4), scales=w1_scales[:], in_=w1_bf[:].rearrange("p t m j -> p (t m j)")
         )
-        h_rows = project("h", w1_words, w1_scales, x_picked, x_picked_scales)
-        gather_edges(2)
-        gather_edges(3)
-        w3_dealt, w3_dealt_scales = deal("w3", w3_raw, w3_plane)
+        h_rows = [project("h", t, w1_words, w1_scales, x_picked, x_picked_scales) for t in range(PACK)]
+        shared = pool.tile([P, 2304], F32, name="shared", tag="reused", align_bytes=64)
+        gather_edges(2, [shared[:, 192:448], shared[:, 640:896]])
+        gather_edges(3, [shared[:, 2048:2304], shared[:, 1088:1344]])
+        w3_dealt = deal_words("w3_dealt", w3_raw)
+        w3_dealt_scales = deal_scales("w3_dealt_scales", w3_plane)
 
-        messages = [[sb("message%d_%d" % (u, d), [P, PACK, HALF], F32) for d in range(2)] for u in range(2)]
+        widths = (192, 64)
+        starts = (64, 0)
+        pieces = (((0, 128), (128, 64)), ((0, 64),))
+        messages = [
+            [sb("message0", [P, PACK, 192], F32)[:], shared[:, :1792].rearrange("p (t v) -> p t v", t=PACK)[:, :, :192]],
+            [shared[:, 1152:2176].rearrange("p (t v) -> p t v", t=PACK)[:, :, 64 * d : 64 * (d + 1)] for d in range(2)],
+        ]
 
         def multiply(u, t):
+            lo, hi = starts[u], starts[u] + widths[u]
             for d in range(2):
                 nc.vector.tensor_tensor(
                     messages[u][d][:, t, :],
-                    h_rows[t][:].indirect(places[d][:, 8 * u : 8 * (u + 1)]),
-                    r_edge[t][d][:, HALF * u : HALF * (u + 1)],
+                    h_rows[t][:].indirect(places[d][:, lo // 16 : hi // 16]),
+                    r_edge[t][d][:, lo:hi],
                     MULT,
                 )
 
-        z_bf = [sb("z_bf" + str(u), [P, HALF * PACK], BF16) for u in range(2)]
-        z_words = [sb("z_words" + str(u), [P, HALF], U32) for u in range(2)]
-        z_scales = [sb("z_scales" + str(u), [P, HALF], U8) for u in range(2)]
-        y_bank = [psum.tile([P, PACK, HALF], F32, name="y_bank" + str(u)) for u in range(2)]
-        y_f32 = [sb("y_f32" + str(u), [P, PACK, HALF], F32) for u in range(2)]
-        y_bf = [sb("y_bf" + str(u), [P, HALF, PACK], BF16) for u in range(2)]
-        y_words = [sb("y_words" + str(u), [P, HALF], I32) for u in range(2)]
+        z_bf = [shared[:, 1664:2048].bitcast(BF16), sb("z_bf", [P, 64 * PACK], BF16)[:]]
+        z_words = [sb("z_words" + str(u), [P, widths[u]], U32) for u in range(2)]
+        z_scales = [sb("z_scales" + str(u), [P, widths[u]], U8) for u in range(2)]
+        y_bank = [
+            [psum.tile([P, PACK, n], F32, name="y_bank%d_%d" % (u, lo)) for lo, n in pieces[u]] for u in range(2)
+        ]
+        y_f32 = [sb("y_f32" + str(u), [P, PACK, widths[u]], F32) for u in range(2)]
+        y_bf = [sb("y_bf" + str(u), [P, widths[u] * PACK], BF16) for u in range(2)]
+        y_words = [sb("y_words" + str(u), [P, widths[u]], I32) for u in range(2)]
         y_scales = sb("y_scales", [P, TARGETS], U8)
         out_rows = out_0.rearrange("(p t) v -> p t v", t=PACK)
         out_words = out_1[0].rearrange("p v t -> p (v t)").bitcast(I32)
 
         def add_messages(u):
             nc.vector.tensor_tensor(
-                z_bf[u][:].rearrange("p (c i t) -> p c t i", t=PACK, i=4),
-                messages[u][0][:].rearrange("p t (c i) -> p c t i", i=4),
-                messages[u][1][:].rearrange("p t (c i) -> p c t i", i=4),
+                z_bf[u].rearrange("p (c i t) -> p c t i", t=PACK, i=4),
+                messages[u][0].rearrange("p t (c i) -> p c t i", i=4),
+                messages[u][1].rearrange("p t (c i) -> p c t i", i=4),
                 ADD,
             )
 
         def last_product(u):
-            nc.vector.quantize_mx(out=z_words[u][:].bitcast(FP8X4), scales=z_scales[u][:], in_=z_bf[u][:])
-            for t in range(PACK):
-                cols = slice(t * P, (t + 1) * P)
-                nc.tensor.matmul_mx(
-                    out=y_bank[u][:, t, :], lhsT=w3_dealt[:, cols].bitcast(FP8X4), lhsT_scale=w3_dealt_scales[:, cols],
-                    rhs=z_words[u][:].bitcast(FP8X4), rhs_scale=z_scales[u][:], start=True, stop=True,
+            for bank, (lo, n) in zip(y_bank[u], pieces[u]):
+                part = slice(lo, lo + n)
+                nc.vector.quantize_mx(
+                    out=z_words[u][:, part].bitcast(FP8X4), scales=z_scales[u][:, part],
+                    in_=z_bf[u][:, PACK * lo : PACK * (lo + n)],
+                )
+                for t in range(PACK):
+                    cols = slice(t * P, (t + 1) * P)
+                    nc.tensor.matmul_mx(
+                        out=bank[:, t, :], lhsT=w3_dealt[:, cols].bitcast(FP8X4), lhsT_scale=w3_dealt_scales[:, cols],
+                        rhs=z_words[u][:, part].bitcast(FP8X4), rhs_scale=z_scales[u][:, part], start=True, stop=True,
+                    )
+
+        def round_result(u, copy):
+            for bank, (lo, n) in zip(y_bank[u], pieces[u]):
+                copy(
+                    y_bf[u][:, PACK * lo : PACK * (lo + n)].rearrange("p (v t) -> p v t", t=PACK),
+                    bank[:].rearrange("p t v -> p v t"),
                 )
 
-        def store_f32(u):
-            nc.scalar.copy(y_f32[u][:], y_bank[u][:])
-            nc.scalar.dma_start(out_rows[:, :, HALF * u : HALF * (u + 1)], y_f32[u][:])
+        def store_result(u):
+            for bank, (lo, n) in zip(y_bank[u], pieces[u]):
+                nc.scalar.copy(y_f32[u][:, :, lo : lo + n], bank[:])
+            nc.scalar.dma_start(out_rows[:, :, starts[u] : starts[u] + widths[u]], y_f32[u][:])
 
         def quantize_result(u):
-            cols = slice(HALF * u, HALF * (u + 1))
-            nc.vector.quantize_mx(
-                out=y_words[u][:].bitcast(FP8X4), scales=y_scales[:, cols], in_=y_bf[u][:].rearrange("p v t -> p (v t)")
-            )
-            nc.sync.dma_start(out_words[:, cols], y_words[u][:])
+            for lo, n in pieces[u]:
+                nc.vector.quantize_mx(
+                    out=y_words[u][:, lo : lo + n].bitcast(FP8X4),
+                    scales=y_scales[:, starts[u] + lo : starts[u] + lo + n],
+                    in_=y_bf[u][:, PACK * lo : PACK * (lo + n)],
+                )
+            nc.sync.dma_start(out_words[:, starts[u] : starts[u] + widths[u]], y_words[u][:])
 
         for t in range(PACK):
             multiply(0, t)
@@ -209,15 +238,15 @@ def tile_picked_zcomp_mul_po_kernel(
         add_messages(0)
         multiply(1, 1)
         last_product(0)
-        nc.scalar.copy(y_bf[0][:], y_bank[0][:].rearrange("p t v -> p v t"))
-        store_f32(0)
+        round_result(0, nc.scalar.copy)
+        store_result(0)
         multiply(1, 2)
         multiply(1, 3)
         add_messages(1)
-        quantize_result(0)
         last_product(1)
-        nc.vector.tensor_copy(y_bf[1][:], y_bank[1][:].rearrange("p t v -> p v t"))
-        store_f32(1)
+        quantize_result(0)
+        round_result(1, nc.vector.tensor_copy)
+        store_result(1)
         quantize_result(1)
         for q in range(4):
             queue = nc.sync if q % 2 else nc.scalar

@@ -52,18 +52,18 @@ def tile_picked_zcomp_mul_po_kernel(
             for q in range(4):
                 queue.dma_start(tile[32 * q : 32 * q + 4, :].bitcast(I32), src[0, 4 * q : 4 * q + 4, :].bitcast(I32))
 
-        def deal_words(name, words):
+        def deal_words(name, words, engine):
             dealt = sb(name, [P, 512], I32)
-            nc.vector.tensor_copy(
+            engine.tensor_copy(
                 dealt[:].rearrange("p (t c i) -> p c t i", t=PACK, i=4),
                 words[:].rearrange("p (c i t) -> p c t i", t=PACK, i=4),
             )
             return dealt
 
-        def deal_scales(name, scales):
+        def deal_scales(name, scales, engine):
             dealt = sb(name, [P, 512], U8)
-            nc.vector.tensor_copy(
-                dealt[:].rearrange("p (t m) -> p m t", t=PACK), scales[:].rearrange("p (m t) -> p m t", t=PACK)
+            engine.tensor_copy(
+                dealt[:].rearrange("p (t m) -> p t m", t=PACK), scales[:].rearrange("p (m t) -> p t m", t=PACK)
             )
             return dealt
 
@@ -113,10 +113,10 @@ def tile_picked_zcomp_mul_po_kernel(
         w3_raw = load_words("w3_raw", w3_words)
         load_scales(w3_plane, w3_scales, nc.sync)
 
-        w2_dealt = deal_words("w2_dealt", w2_raw)
+        w2_dealt = deal_words("w2_dealt", w2_raw, nc.vector)
         e_picked_scales = gather_scales("e_picked_scales", e_plane, attr_sb)
         e_picked = gather_words("e_picked", e_table, attr_sb)
-        w2_dealt_scales = deal_scales("w2_dealt_scales", w2_plane)
+        w2_dealt_scales = deal_scales("w2_dealt_scales", w2_plane, nc.vector)
 
         w1_bf = pool.tile([P, PACK, P, PACK], BF16, name="w1_bf", tag="reused", align_bytes=64)
 
@@ -155,8 +155,8 @@ def tile_picked_zcomp_mul_po_kernel(
         shared = pool.tile([P, 2304], F32, name="shared", tag="reused", align_bytes=64)
         gather_edges(2, [shared[:, 192:448], shared[:, 640:896]])
         gather_edges(3, [shared[:, 2048:2304], shared[:, 1088:1344]])
-        w3_dealt = deal_words("w3_dealt", w3_raw)
-        w3_dealt_scales = deal_scales("w3_dealt_scales", w3_plane)
+        w3_dealt = deal_words("w3_dealt", w3_raw, nc.gpsimd)
+        w3_dealt_scales = deal_scales("w3_dealt_scales", w3_plane, nc.gpsimd)
 
         widths = (192, 64)
         starts = (64, 0)

@@ -30,8 +30,8 @@ def tile_picked_zcomp_mul_po_kernel(
         pool = ctx.enter_context(tc.tile_pool(name="sbuf", bufs=1))
         psum = ctx.enter_context(tc.psum_pool(name="psum", bufs=1))
 
-        def sb(name, shape, dtype):
-            return pool.tile(shape, dtype, name=name, align_bytes=64)
+        def sb(name, shape, dtype, tag=None):
+            return pool.tile(shape, dtype, name=name, tag=tag or name, align_bytes=64)
 
         def load_list(name, src):
             tile = pool.tile(list(src.shape), U16, name=name)
@@ -60,32 +60,33 @@ def tile_picked_zcomp_mul_po_kernel(
             )
             return dealt
 
-        def deal_scales(name, scales, engine):
+        def deal_scales(name, scales, cuts):
             dealt = sb(name, [P, 512], U8)
-            engine.tensor_copy(
-                dealt[:].rearrange("p (t m) -> p t m", t=PACK), scales[:].rearrange("p (m t) -> p t m", t=PACK)
-            )
+            for lo, hi in cuts:
+                nc.gpsimd.tensor_copy(
+                    dealt[:].rearrange("p (t m) -> p t m", t=PACK)[:, lo:hi, :],
+                    scales[:].rearrange("p (m t) -> p t m", t=PACK)[:, lo:hi, :],
+                )
             return dealt
 
-        def gather_words(name, words, offsets):
-            picked = sb(name, [P, PICKED], U32)
+        def gather_words(name, words, offsets, tag=None):
+            picked = sb(name, [P, PICKED], U32, tag)
             nc.vector.tensor_copy(picked[:], words[:].bitcast(U32).indirect(offsets[:]))
             return picked
 
-        def gather_scales(name, scales, offsets):
-            picked = sb(name, [P, PICKED], U8)
+        def gather_scales(name, scales, offsets, tag=None):
+            picked = sb(name, [P, PICKED], U8, tag)
             nc.vector.tensor_copy(picked[:], scales[:].indirect(offsets[:]))
             return picked
 
-        def project(name, t, w_words, w_scales, words, scales):
+        def project(row, t, w_words, w_scales, words, scales):
             cols = slice(t * P, (t + 1) * P)
             bank = psum.tile([P, PICKED], F32, name="bank", tag="bank", bufs=5)
             nc.tensor.matmul_mx(
                 out=bank[:], lhsT=w_words[:, cols].bitcast(FP8X4), lhsT_scale=w_scales[:, cols],
                 rhs=words[:].bitcast(FP8X4), rhs_scale=scales[:], start=True, stop=True,
             )
-            row = pool.tile([P, PICKED], F32, name=name + str(t), tag=name + str(t), align_bytes=64)
-            nc.scalar.copy(row[:], bank[:])
+            nc.scalar.copy(row, bank[:])
             return row
 
         e_plane = cleared_plane("e_plane", TABLE)
@@ -97,13 +98,13 @@ def tile_picked_zcomp_mul_po_kernel(
         attr_sb = load_list("attr_sb", attr)
         load_scales(e_plane, e_scales, nc.sync)
         e_table = load_words("e_table", e_words)
+        x_table = load_words("x_table", x_words)
         load_scales(w2_plane, w2_scales, nc.sync)
         offs_sb = load_list("offs_sb", offs)
-        x_table = load_words("x_table", x_words)
         w1_rows = w1.rearrange("(p j) c -> p j c", j=PACK)
         w1_raw = []
         for u in range(2):
-            part = sb("w1_raw" + str(u), [P, PACK, 256], F32)
+            part = pool.tile([P, PACK, 256], F32, name="w1_raw" + str(u), tag="w1_raw" + str(u), align_bytes=64)
             nc.sync.dma_start(part[:], w1_rows[:, :, 256 * u : 256 * (u + 1)])
             w1_raw.append(part)
             if u == 0:
@@ -116,7 +117,7 @@ def tile_picked_zcomp_mul_po_kernel(
         w2_dealt = deal_words("w2_dealt", w2_raw, nc.vector)
         e_picked_scales = gather_scales("e_picked_scales", e_plane, attr_sb)
         e_picked = gather_words("e_picked", e_table, attr_sb)
-        w2_dealt_scales = deal_scales("w2_dealt_scales", w2_plane, nc.vector)
+        w2_dealt_scales = deal_scales("w2_dealt_scales", w2_plane, ((0, 2), (2, 4)))
 
         w1_bf = pool.tile([P, PACK, P, PACK], BF16, name="w1_bf", tag="reused", align_bytes=64)
 
@@ -126,13 +127,15 @@ def tile_picked_zcomp_mul_po_kernel(
                 w1_raw[s // 2][:, :, 128 * (s % 2) : 128 * (s % 2 + 1)].rearrange("p j (m t) -> p m t j", t=PACK),
             )
 
-        round_w1(0)
-        round_w1(1)
-        r_rows = []
-        for t in range(PACK):
-            r_rows.append(project("r", t, w2_dealt, w2_dealt_scales, e_picked, e_picked_scales))
-            if t < 2:
-                round_w1(2 + t)
+        def own_row(name):
+            return pool.tile([P, PICKED], F32, name=name, tag=name, align_bytes=64)[:]
+
+        r_rows = [project(own_row("r" + str(t)), t, w2_dealt, w2_dealt_scales, e_picked, e_picked_scales) for t in range(2)]
+        for s in range(4):
+            round_w1(s)
+        late_rows = pool.tile([P, 2, PICKED], F32, name="late_rows", tag="w1_raw1", align_bytes=64)
+        for t in range(2, PACK):
+            r_rows.append(project(late_rows[:, t - 2, :], t, w2_dealt, w2_dealt_scales, e_picked, e_picked_scales))
 
         x_picked = gather_words("x_picked", x_table, offs_sb)
         x_picked_scales = gather_scales("x_picked_scales", x_plane, offs_sb)
@@ -141,22 +144,22 @@ def tile_picked_zcomp_mul_po_kernel(
 
         def gather_edges(t, rooms):
             for d in range(2):
-                nc.vector.tensor_copy(rooms[d], r_rows[t][:].indirect(edges[d][:]))
+                nc.vector.tensor_copy(rooms[d], r_rows[t].indirect(edges[d][:]))
             r_edge.append(rooms)
 
         for t in range(2):
             gather_edges(t, [sb("r_edge%d_%d" % (t, d), [P, TARGETS], F32)[:] for d in range(2)])
-        w1_words = pool.tile([P, 512], U32, name="w1_words", tag="r0", align_bytes=64)
+        w1_words = pool.tile([P, 512], U32, name="w1_words", align_bytes=64)
         w1_scales = sb("w1_scales", [P, 512], U8)
         nc.vector.quantize_mx(
             out=w1_words[:].bitcast(FP8X4), scales=w1_scales[:], in_=w1_bf[:].rearrange("p t m j -> p (t m j)")
         )
-        h_rows = [project("h", t, w1_words, w1_scales, x_picked, x_picked_scales) for t in range(PACK)]
-        shared = pool.tile([P, 2304], F32, name="shared", tag="reused", align_bytes=64)
+        h_rows = [project(own_row("h" + str(t)), t, w1_words, w1_scales, x_picked, x_picked_scales) for t in range(PACK)]
+        shared = pool.tile([P, 2304], F32, name="shared", align_bytes=64)
         gather_edges(2, [shared[:, 192:448], shared[:, 640:896]])
         gather_edges(3, [shared[:, 2048:2304], shared[:, 1088:1344]])
         w3_dealt = deal_words("w3_dealt", w3_raw, nc.gpsimd)
-        w3_dealt_scales = deal_scales("w3_dealt_scales", w3_plane, nc.gpsimd)
+        w3_dealt_scales = deal_scales("w3_dealt_scales", w3_plane, ((0, 4),))
 
         widths = (192, 64)
         starts = (64, 0)
@@ -171,7 +174,7 @@ def tile_picked_zcomp_mul_po_kernel(
             for d in range(2):
                 nc.vector.tensor_tensor(
                     messages[u][d][:, t, :],
-                    h_rows[t][:].indirect(places[d][:, lo // 16 : hi // 16]),
+                    h_rows[t].indirect(places[d][:, lo // 16 : hi // 16]),
                     r_edge[t][d][:, lo:hi],
                     MULT,
                 )

@@ -28,6 +28,7 @@ def tile_picked_zcomp_mul_po_kernel(
     nc = tc.nc
     with ExitStack() as ctx:
         pool = ctx.enter_context(tc.tile_pool(name="sbuf", bufs=1))
+        reused = ctx.enter_context(tc.tile_pool(name="reused", bufs=1))
         psum = ctx.enter_context(tc.psum_pool(name="psum", bufs=1))
 
         def sb(name, shape, dtype, tag=None):
@@ -48,20 +49,18 @@ def tile_picked_zcomp_mul_po_kernel(
             nc.vector.memset(tile[:].bitcast(I32), 0)
             return tile
 
-        def load_scales(tile, src, queue):
-            for q in range(4):
-                queue.dma_start(tile[32 * q : 32 * q + 4, :].bitcast(I32), src[0, 4 * q : 4 * q + 4, :].bitcast(I32))
+        def load_scales(tile, src, queues, quadrants=range(4)):
+            for q in quadrants:
+                queues[q % len(queues)].dma_start(tile[32 * q : 32 * q + 4, :].bitcast(I32), src[0, 4 * q : 4 * q + 4, :].bitcast(I32))
 
-        def deal_words(name, words, engine):
-            dealt = sb(name, [P, 512], I32)
+        def deal_words(dealt, words, engine):
             engine.tensor_copy(
                 dealt[:].rearrange("p (t c i) -> p c t i", t=PACK, i=4),
                 words[:].rearrange("p (c i t) -> p c t i", t=PACK, i=4),
             )
             return dealt
 
-        def deal_scales(name, scales, cuts):
-            dealt = sb(name, [P, 512], U8)
+        def deal_scales(dealt, scales, cuts):
             for lo, hi in cuts:
                 nc.gpsimd.tensor_copy(
                     dealt[:].rearrange("p (t m) -> p t m", t=PACK)[:, lo:hi, :],
@@ -90,17 +89,19 @@ def tile_picked_zcomp_mul_po_kernel(
             return row
 
         e_plane = cleared_plane("e_plane", TABLE)
-        w2_plane = cleared_plane("w2_plane", 512)
         x_plane = cleared_plane("x_plane", TABLE)
+        w2_plane = cleared_plane("w2_plane", 512)
         w3_plane = cleared_plane("w3_plane", 512)
 
         w2_raw = load_words("w2_raw", w2_words)
         attr_sb = load_list("attr_sb", attr)
-        load_scales(e_plane, e_scales, nc.sync)
+        load_scales(e_plane, e_scales, (nc.scalar, nc.sync))
         e_table = load_words("e_table", e_words)
         x_table = load_words("x_table", x_words)
-        load_scales(w2_plane, w2_scales, nc.sync)
+        load_scales(x_plane, x_scales, (nc.gpsimd,), range(2))
+        load_scales(w2_plane, w2_scales, (nc.sync,))
         offs_sb = load_list("offs_sb", offs)
+        load_scales(x_plane, x_scales, (nc.sync,), range(2, 4))
         w1_rows = w1.rearrange("(p j) c -> p j c", j=PACK)
         w1_raw = []
         for u in range(2):
@@ -108,18 +109,17 @@ def tile_picked_zcomp_mul_po_kernel(
             nc.sync.dma_start(part[:], w1_rows[:, :, 256 * u : 256 * (u + 1)])
             w1_raw.append(part)
             if u == 0:
-                load_scales(x_plane, x_scales, nc.sync)
                 edges = [load_list("edge1_sb", edge1), load_list("edge2_sb", edge2)]
         places = [load_list("pos1_sb", pos1), load_list("pos2_sb", pos2)]
         w3_raw = load_words("w3_raw", w3_words)
-        load_scales(w3_plane, w3_scales, nc.sync)
+        load_scales(w3_plane, w3_scales, (nc.sync,))
 
-        w2_dealt = deal_words("w2_dealt", w2_raw, nc.vector)
+        w2_dealt = deal_words(sb("w2_dealt", [P, 512], I32), w2_raw, nc.vector)
         e_picked_scales = gather_scales("e_picked_scales", e_plane, attr_sb)
         e_picked = gather_words("e_picked", e_table, attr_sb)
-        w2_dealt_scales = deal_scales("w2_dealt_scales", w2_plane, ((0, 2), (2, 4)))
+        w2_dealt_scales = deal_scales(sb("w2_dealt_scales", [P, 512], U8), w2_plane, ((0, 2), (2, 4)))
 
-        w1_bf = pool.tile([P, PACK, P, PACK], BF16, name="w1_bf", tag="reused", align_bytes=64)
+        w1_bf = reused.tile([P, PACK, P, PACK], BF16, name="w1_bf", align_bytes=64, offset=0)
 
         def round_w1(s):
             nc.scalar.copy(
@@ -158,8 +158,8 @@ def tile_picked_zcomp_mul_po_kernel(
         shared = pool.tile([P, 2304], F32, name="shared", align_bytes=64)
         gather_edges(2, [shared[:, 192:448], shared[:, 640:896]])
         gather_edges(3, [shared[:, 2048:2304], shared[:, 1088:1344]])
-        w3_dealt = deal_words("w3_dealt", w3_raw, nc.gpsimd)
-        w3_dealt_scales = deal_scales("w3_dealt_scales", w3_plane, ((0, 4),))
+        w3_dealt = deal_words(reused.tile([P, 512], I32, name="w3_dealt", align_bytes=64, offset=0), w3_raw, nc.gpsimd)
+        w3_dealt_scales = deal_scales(reused.tile([P, 512], U8, name="w3_dealt_scales", align_bytes=64, offset=2048), w3_plane, ((0, 4),))
 
         widths = (192, 64)
         starts = (64, 0)
@@ -241,14 +241,14 @@ def tile_picked_zcomp_mul_po_kernel(
         add_messages(0)
         multiply(1, 1)
         last_product(0)
-        round_result(0, nc.scalar.copy)
         store_result(0)
+        round_result(0, nc.scalar.copy)
         multiply(1, 2)
         multiply(1, 3)
         add_messages(1)
         last_product(1)
         quantize_result(0)
-        round_result(1, nc.vector.tensor_copy)
+        round_result(1, nc.scalar.copy)
         store_result(1)
         quantize_result(1)
         for q in range(4):

@@ -102,14 +102,14 @@ def tile_picked_zcomp_mul_po_kernel(
         load_scales(w2_plane, w2_scales, (nc.sync,))
         offs_sb = load_list("offs_sb", offs)
         load_scales(x_plane, x_scales, (nc.sync,), range(2, 4))
+        edges = [load_list("edge1_sb", edge1), load_list("edge2_sb", edge2)]
         w1_rows = w1.rearrange("(p j) c -> p j c", j=PACK)
         w1_raw = []
-        for u in range(2):
-            part = pool.tile([P, PACK, 256], F32, name="w1_raw" + str(u), tag="w1_raw" + str(u), align_bytes=64)
-            nc.sync.dma_start(part[:], w1_rows[:, :, 256 * u : 256 * (u + 1)])
+        w1_cuts = ((0, 320), (320, 512))
+        for u, (lo, hi) in enumerate(w1_cuts):
+            part = pool.tile([P, PACK, hi - lo], F32, name="w1_raw" + str(u), tag="w1_raw" + str(u), align_bytes=64)
+            nc.sync.dma_start(part[:], w1_rows[:, :, lo:hi])
             w1_raw.append(part)
-            if u == 0:
-                edges = [load_list("edge1_sb", edge1), load_list("edge2_sb", edge2)]
         places = [load_list("pos1_sb", pos1), load_list("pos2_sb", pos2)]
         w3_raw = load_words("w3_raw", w3_words)
         load_scales(w3_plane, w3_scales, (nc.sync,))
@@ -121,18 +121,21 @@ def tile_picked_zcomp_mul_po_kernel(
 
         w1_bf = reused.tile([P, PACK, P, PACK], BF16, name="w1_bf", align_bytes=64, offset=0)
 
-        def round_w1(s):
-            nc.scalar.copy(
-                w1_bf[:, :, 32 * s : 32 * (s + 1), :].rearrange("p t m j -> p m t j"),
-                w1_raw[s // 2][:, :, 128 * (s % 2) : 128 * (s % 2 + 1)].rearrange("p j (m t) -> p m t j", t=PACK),
+        def round_w1(copy, u, lo, hi):
+            first = w1_cuts[u][0]
+            copy(
+                w1_bf[:, :, lo // PACK : hi // PACK, :].rearrange("p t m j -> p m t j"),
+                w1_raw[u][:, :, lo - first : hi - first].rearrange("p j (m t) -> p m t j", t=PACK),
             )
 
         def own_row(name):
             return pool.tile([P, PICKED], F32, name=name, tag=name, align_bytes=64)[:]
 
         r_rows = [project(own_row("r" + str(t)), t, w2_dealt, w2_dealt_scales, e_picked, e_picked_scales) for t in range(2)]
-        for s in range(4):
-            round_w1(s)
+        round_w1(nc.gpsimd.tensor_copy, 0, 0, 128)
+        round_w1(nc.scalar.copy, 0, 128, 320)
+        round_w1(nc.scalar.copy, 1, 320, 448)
+        round_w1(nc.gpsimd.tensor_copy, 1, 448, 512)
         late_rows = pool.tile([P, 2, PICKED], F32, name="late_rows", tag="w1_raw1", align_bytes=64)
         for t in range(2, PACK):
             r_rows.append(project(late_rows[:, t - 2, :], t, w2_dealt, w2_dealt_scales, e_picked, e_picked_scales))

@@ -158,18 +158,21 @@ def tile_picked_zcomp_mul_po_kernel(
             out=w1_words[:].bitcast(FP8X4), scales=w1_scales[:], in_=w1_bf[:].rearrange("p t m j -> p (t m j)")
         )
         h_rows = [project(own_row("h" + str(t)), t, w1_words, w1_scales, x_picked, x_picked_scales) for t in range(PACK)]
-        shared = pool.tile([P, 2304], F32, name="shared", align_bytes=64)
-        gather_edges(2, [shared[:, 192:448], shared[:, 640:896]])
-        gather_edges(3, [shared[:, 2048:2304], shared[:, 1088:1344]])
+        unit = 64
+        base = 28 * unit
+        shared = sb("shared", [P, 48 * unit], F32)
+        gather_edges(2, [sb("r_edge2_%d" % d, [P, TARGETS], F32)[:] for d in range(2)])
+        gather_edges(3, [shared[:, base + (4 * d - 1) * unit : base + (4 * d + 3) * unit] for d in range(2)])
         w3_dealt = deal_words(reused.tile([P, 512], I32, name="w3_dealt", align_bytes=64, offset=0), w3_raw, nc.gpsimd)
         w3_dealt_scales = deal_scales(reused.tile([P, 512], U8, name="w3_dealt_scales", align_bytes=64, offset=2048), w3_plane, ((0, 4),))
 
         widths = (192, 64)
         starts = (64, 0)
-        pieces = (((0, 128), (128, 64)), ((0, 64),))
+        pieces = ((0, 0, 128), (0, 128, 64), (1, 0, 64))
+        narrow = shared[:, base : base + 16 * unit].rearrange("p (t v) -> p t v", t=PACK)
         messages = [
-            [sb("message0", [P, PACK, 192], F32)[:], shared[:, :1792].rearrange("p (t v) -> p t v", t=PACK)[:, :, :192]],
-            [shared[:, 1152:2176].rearrange("p (t v) -> p t v", t=PACK)[:, :, 64 * d : 64 * (d + 1)] for d in range(2)],
+            [sb("message0", [P, PACK, 192], F32)[:], shared[:].rearrange("p (t v) -> p t v", t=PACK)[:, :, :192]],
+            [narrow[:, :, unit * d : unit * (d + 1)] for d in range(2)],
         ]
 
         def multiply(u, t):
@@ -182,12 +185,10 @@ def tile_picked_zcomp_mul_po_kernel(
                     MULT,
                 )
 
-        z_bf = [shared[:, 1664:2048].bitcast(BF16), sb("z_bf", [P, 64 * PACK], BF16)[:]]
+        z_bf = [shared[:, base + 12 * unit : base + 18 * unit].bitcast(BF16), sb("z_bf", [P, 64 * PACK], BF16)[:]]
         z_words = [sb("z_words" + str(u), [P, widths[u]], U32) for u in range(2)]
         z_scales = [sb("z_scales" + str(u), [P, widths[u]], U8) for u in range(2)]
-        y_bank = [
-            [psum.tile([P, PACK, n], F32, name="y_bank%d_%d" % (u, lo)) for lo, n in pieces[u]] for u in range(2)
-        ]
+        y_bank = [psum.tile([P, PACK, n], F32, name="y_bank%d_%d" % (u, lo)) for u, lo, n in pieces]
         y_f32 = [sb("y_f32" + str(u), [P, PACK, widths[u]], F32) for u in range(2)]
         y_bf = [sb("y_bf" + str(u), [P, widths[u] * PACK], BF16) for u in range(2)]
         y_words = [sb("y_words" + str(u), [P, widths[u]], I32) for u in range(2)]
@@ -195,65 +196,79 @@ def tile_picked_zcomp_mul_po_kernel(
         out_rows = out_0.rearrange("(p t) v -> p t v", t=PACK)
         out_words = out_1[0].rearrange("p v t -> p (v t)").bitcast(I32)
 
-        def add_messages(u):
+        def add_messages(k):
+            u, lo, n = pieces[k]
             nc.vector.tensor_tensor(
-                z_bf[u].rearrange("p (c i t) -> p c t i", t=PACK, i=4),
-                messages[u][0].rearrange("p t (c i) -> p c t i", i=4),
-                messages[u][1].rearrange("p t (c i) -> p c t i", i=4),
+                z_bf[u][:, PACK * lo : PACK * (lo + n)].rearrange("p (c i t) -> p c t i", t=PACK, i=4),
+                messages[u][0][:, :, lo : lo + n].rearrange("p t (c i) -> p c t i", i=4),
+                messages[u][1][:, :, lo : lo + n].rearrange("p t (c i) -> p c t i", i=4),
                 ADD,
             )
 
-        def last_product(u):
-            for bank, (lo, n) in zip(y_bank[u], pieces[u]):
-                part = slice(lo, lo + n)
-                nc.vector.quantize_mx(
-                    out=z_words[u][:, part].bitcast(FP8X4), scales=z_scales[u][:, part],
-                    in_=z_bf[u][:, PACK * lo : PACK * (lo + n)],
-                )
-                for t in range(PACK):
-                    cols = slice(t * P, (t + 1) * P)
-                    nc.tensor.matmul_mx(
-                        out=bank[:, t, :], lhsT=w3_dealt[:, cols].bitcast(FP8X4), lhsT_scale=w3_dealt_scales[:, cols],
-                        rhs=z_words[u][:, part].bitcast(FP8X4), rhs_scale=z_scales[u][:, part], start=True, stop=True,
-                    )
-
-        def round_result(u, copy):
-            for bank, (lo, n) in zip(y_bank[u], pieces[u]):
-                copy(
-                    y_bf[u][:, PACK * lo : PACK * (lo + n)].rearrange("p (v t) -> p v t", t=PACK),
-                    bank[:].rearrange("p t v -> p v t"),
+        def last_product(k):
+            u, lo, n = pieces[k]
+            part = slice(lo, lo + n)
+            nc.vector.quantize_mx(
+                out=z_words[u][:, part].bitcast(FP8X4), scales=z_scales[u][:, part],
+                in_=z_bf[u][:, PACK * lo : PACK * (lo + n)],
+            )
+            for t in range(PACK):
+                cols = slice(t * P, (t + 1) * P)
+                nc.tensor.matmul_mx(
+                    out=y_bank[k][:, t, :], lhsT=w3_dealt[:, cols].bitcast(FP8X4), lhsT_scale=w3_dealt_scales[:, cols],
+                    rhs=z_words[u][:, part].bitcast(FP8X4), rhs_scale=z_scales[u][:, part], start=True, stop=True,
                 )
 
-        def store_result(u):
-            for bank, (lo, n) in zip(y_bank[u], pieces[u]):
-                nc.scalar.copy(y_f32[u][:, :, lo : lo + n], bank[:])
-            nc.scalar.dma_start(out_rows[:, :, starts[u] : starts[u] + widths[u]], y_f32[u][:])
+        def round_result(k):
+            u, lo, n = pieces[k]
+            nc.scalar.copy(
+                y_bf[u][:, PACK * lo : PACK * (lo + n)].rearrange("p (v t) -> p v t", t=PACK),
+                y_bank[k][:].rearrange("p t v -> p v t"),
+            )
 
-        def quantize_result(u):
-            for lo, n in pieces[u]:
-                nc.vector.quantize_mx(
-                    out=y_words[u][:, lo : lo + n].bitcast(FP8X4),
-                    scales=y_scales[:, starts[u] + lo : starts[u] + lo + n],
-                    in_=y_bf[u][:, PACK * lo : PACK * (lo + n)],
-                )
+        def fetch_result(k):
+            u, lo, n = pieces[k]
+            nc.scalar.copy(y_f32[u][:, :, lo : lo + n], y_bank[k][:])
+
+        def store_result(u, queue):
+            queue.dma_start(out_rows[:, :, starts[u] : starts[u] + widths[u]], y_f32[u][:])
+
+        def quantize_result(k):
+            u, lo, n = pieces[k]
+            nc.vector.quantize_mx(
+                out=y_words[u][:, lo : lo + n].bitcast(FP8X4),
+                scales=y_scales[:, starts[u] + lo : starts[u] + lo + n],
+                in_=y_bf[u][:, PACK * lo : PACK * (lo + n)],
+            )
+
+        def store_words(u):
             nc.sync.dma_start(out_words[:, starts[u] : starts[u] + widths[u]], y_words[u][:])
 
         for t in range(PACK):
             multiply(0, t)
         multiply(1, 0)
         add_messages(0)
-        multiply(1, 1)
+        add_messages(1)
         last_product(0)
-        store_result(0)
-        round_result(0, nc.scalar.copy)
+        multiply(1, 1)
+        last_product(1)
+        fetch_result(0)
+        fetch_result(1)
+        store_result(0, nc.sync)
+        round_result(0)
+        round_result(1)
         multiply(1, 2)
         multiply(1, 3)
-        add_messages(1)
-        last_product(1)
+        add_messages(2)
+        last_product(2)
         quantize_result(0)
-        round_result(1, nc.scalar.copy)
-        store_result(1)
         quantize_result(1)
+        store_words(0)
+        round_result(2)
+        fetch_result(2)
+        store_result(1, nc.scalar)
+        quantize_result(2)
+        store_words(1)
         for q in range(4):
             queue = nc.sync if q % 2 else nc.scalar
             queue.dma_start(out_2[0, 4 * q : 4 * q + 4, :].bitcast(I32), y_scales[32 * q : 32 * q + 4, :].bitcast(I32))

@@ -190,8 +190,8 @@ def tile_picked_zcomp_mul_po_kernel(
         z_scales = [sb("z_scales" + str(u), [P, widths[u]], U8) for u in range(2)]
         y_bank = [psum.tile([P, PACK, n], F32, name="y_bank%d_%d" % (u, lo)) for u, lo, n in pieces]
         y_f32 = [sb("y_f32" + str(u), [P, PACK, widths[u]], F32) for u in range(2)]
-        y_bf = [sb("y_bf" + str(u), [P, widths[u] * PACK], BF16) for u in range(2)]
-        y_words = [sb("y_words" + str(u), [P, widths[u]], I32) for u in range(2)]
+        y_bf = [shared[:, base : base + 4 * unit].bitcast(BF16)] + [sb("y_bf" + str(k), [P, 64 * PACK], BF16)[:] for k in (1, 2)]
+        y_words = sb("y_words", [P, TARGETS], I32)
         y_scales = sb("y_scales", [P, TARGETS], U8)
         out_rows = out_0.rearrange("(p t) v -> p t v", t=PACK)
         out_words = out_1[0].rearrange("p v t -> p (v t)").bitcast(I32)
@@ -220,10 +220,16 @@ def tile_picked_zcomp_mul_po_kernel(
                 )
 
         def round_result(k):
-            u, lo, n = pieces[k]
             nc.scalar.copy(
-                y_bf[u][:, PACK * lo : PACK * (lo + n)].rearrange("p (v t) -> p v t", t=PACK),
+                y_bf[k].rearrange("p (v t) -> p v t", t=PACK),
                 y_bank[k][:].rearrange("p t v -> p v t"),
+            )
+
+        def round_fetched(k):
+            u, lo, n = pieces[k]
+            nc.vector.tensor_copy(
+                y_bf[k].rearrange("p (c i t) -> p c t i", t=PACK, i=4),
+                y_f32[u][:, :, lo : lo + n].rearrange("p t (c i) -> p c t i", i=4),
             )
 
         def fetch_result(k):
@@ -236,13 +242,10 @@ def tile_picked_zcomp_mul_po_kernel(
         def quantize_result(k):
             u, lo, n = pieces[k]
             nc.vector.quantize_mx(
-                out=y_words[u][:, lo : lo + n].bitcast(FP8X4),
+                out=y_words[:, starts[u] + lo : starts[u] + lo + n].bitcast(FP8X4),
                 scales=y_scales[:, starts[u] + lo : starts[u] + lo + n],
-                in_=y_bf[u][:, PACK * lo : PACK * (lo + n)],
+                in_=y_bf[k],
             )
-
-        def store_words(u):
-            nc.sync.dma_start(out_words[:, starts[u] : starts[u] + widths[u]], y_words[u][:])
 
         for t in range(PACK):
             multiply(0, t)
@@ -255,20 +258,19 @@ def tile_picked_zcomp_mul_po_kernel(
         fetch_result(0)
         fetch_result(1)
         store_result(0, nc.sync)
-        round_result(0)
         round_result(1)
         multiply(1, 2)
         multiply(1, 3)
         add_messages(2)
         last_product(2)
-        quantize_result(0)
+        round_fetched(0)
         quantize_result(1)
-        store_words(0)
+        quantize_result(0)
         round_result(2)
         fetch_result(2)
         store_result(1, nc.scalar)
         quantize_result(2)
-        store_words(1)
+        nc.sync.dma_start(out_words, y_words[:])
         for q in range(4):
             queue = nc.sync if q % 2 else nc.scalar
             queue.dma_start(out_2[0, 4 * q : 4 * q + 4, :].bitcast(I32), y_scales[32 * q : 32 * q + 4, :].bitcast(I32))

@@ -114,7 +114,7 @@ def tile_picked_zcomp_mul_po_kernel(
         w3_raw = load_words("w3_raw", w3_words)
         load_scales(w3_plane, w3_scales, (nc.sync,))
 
-        w2_dealt = deal_words(sb("w2_dealt", [P, 512], I32), w2_raw, nc.vector)
+        w2_dealt = deal_words(sb("w2_dealt", [P, 512], I32), w2_raw, nc.gpsimd)
         e_picked_scales = gather_scales("e_picked_scales", e_plane, attr_sb)
         e_picked = gather_words("e_picked", e_table, attr_sb)
         w2_dealt_scales = deal_scales(sb("w2_dealt_scales", [P, 512], U8), w2_plane, ((0, 2), (2, 4)))

@@ -168,7 +168,7 @@ def tile_picked_zcomp_mul_po_kernel(
 
         widths = (192, 64)
         starts = (64, 0)
-        pieces = ((0, 0, 128), (0, 128, 64), (1, 0, 64))
+        pieces = ((0, 64, 128), (0, 0, 64), (1, 0, 64))
         narrow = shared[:, base : base + 16 * unit].rearrange("p (t v) -> p t v", t=PACK)
         messages = [
             [sb("message0", [P, PACK, 192], F32)[:], shared[:].rearrange("p (t v) -> p t v", t=PACK)[:, :, :192]],
@@ -188,8 +188,14 @@ def tile_picked_zcomp_mul_po_kernel(
         z_bf = [shared[:, base + 12 * unit : base + 18 * unit].bitcast(BF16), sb("z_bf", [P, 64 * PACK], BF16)[:]]
         z_words = [sb("z_words" + str(u), [P, widths[u]], U32) for u in range(2)]
         z_scales = [sb("z_scales" + str(u), [P, widths[u]], U8) for u in range(2)]
-        y_bank = [psum.tile([P, PACK, n], F32, name="y_bank%d_%d" % (u, lo)) for u, lo, n in pieces]
-        y_f32 = [sb("y_f32" + str(u), [P, PACK, widths[u]], F32) for u in range(2)]
+        y_bank = [psum.tile([P, PACK, n], F32, name="y_bank%d_%d" % (u, lo))[:] for u, lo, n in pieces[:2]]
+        last_banks = [psum.tile([P, 2, 64], F32, name="last_bank" + str(pair), tag="bank", bufs=5)[:] for pair in range(2)]
+
+        def result_rows(k, t):
+            return y_bank[k][:, t, :] if k < 2 else last_banks[t // 2][:, t % 2, :]
+
+        y_f32 = [sb("y_f32" + str(k), [P, PACK, pieces[k][2]], F32) for k in range(2)]
+        last_f32 = [sb("last_f32" + str(pair), [P, 2, 64], F32) for pair in range(2)]
         y_bf = [shared[:, base : base + 4 * unit].bitcast(BF16)] + [sb("y_bf" + str(k), [P, 64 * PACK], BF16)[:] for k in (1, 2)]
         y_words = sb("y_words", [P, TARGETS], I32)
         y_scales = sb("y_scales", [P, TARGETS], U8)
@@ -215,29 +221,36 @@ def tile_picked_zcomp_mul_po_kernel(
             for t in range(PACK):
                 cols = slice(t * P, (t + 1) * P)
                 nc.tensor.matmul_mx(
-                    out=y_bank[k][:, t, :], lhsT=w3_dealt[:, cols].bitcast(FP8X4), lhsT_scale=w3_dealt_scales[:, cols],
+                    out=result_rows(k, t), lhsT=w3_dealt[:, cols].bitcast(FP8X4), lhsT_scale=w3_dealt_scales[:, cols],
                     rhs=z_words[u][:, part].bitcast(FP8X4), rhs_scale=z_scales[u][:, part], start=True, stop=True,
                 )
 
         def round_result(k):
             nc.scalar.copy(
                 y_bf[k].rearrange("p (v t) -> p v t", t=PACK),
-                y_bank[k][:].rearrange("p t v -> p v t"),
+                y_bank[k].rearrange("p t v -> p v t"),
             )
 
         def round_fetched(k):
-            u, lo, n = pieces[k]
             nc.vector.tensor_copy(
                 y_bf[k].rearrange("p (c i t) -> p c t i", t=PACK, i=4),
-                y_f32[u][:, :, lo : lo + n].rearrange("p t (c i) -> p c t i", i=4),
+                y_f32[k][:].rearrange("p t (c i) -> p c t i", i=4),
             )
 
         def fetch_result(k):
             u, lo, n = pieces[k]
-            nc.scalar.copy(y_f32[u][:, :, lo : lo + n], y_bank[k][:])
+            nc.scalar.copy(y_f32[k][:], y_bank[k])
+            nc.sync.dma_start(out_rows[:, :, starts[u] + lo : starts[u] + lo + n], y_f32[k][:])
 
-        def store_result(u, queue):
-            queue.dma_start(out_rows[:, :, starts[u] : starts[u] + widths[u]], y_f32[u][:])
+        def round_pair(pair, copy):
+            copy(
+                y_bf[2].rearrange("p (v t) -> p v t", t=PACK)[:, :, 2 * pair : 2 * pair + 2],
+                last_banks[pair].rearrange("p t v -> p v t"),
+            )
+
+        def fetch_pair(pair, copy, queue):
+            copy(last_f32[pair][:], last_banks[pair])
+            queue.dma_start(out_rows[:, 2 * pair : 2 * pair + 2, :64], last_f32[pair][:])
 
         def quantize_result(k):
             u, lo, n = pieces[k]
@@ -257,7 +270,6 @@ def tile_picked_zcomp_mul_po_kernel(
         last_product(1)
         fetch_result(0)
         fetch_result(1)
-        store_result(0, nc.sync)
         round_result(1)
         multiply(1, 2)
         multiply(1, 3)
@@ -266,9 +278,10 @@ def tile_picked_zcomp_mul_po_kernel(
         round_fetched(0)
         quantize_result(1)
         quantize_result(0)
-        round_result(2)
-        fetch_result(2)
-        store_result(1, nc.scalar)
+        round_pair(0, nc.vector.tensor_copy)
+        round_pair(1, nc.scalar.copy)
+        fetch_pair(0, nc.vector.tensor_copy, nc.sync)
+        fetch_pair(1, nc.scalar.copy, nc.scalar)
         quantize_result(2)
         nc.sync.dma_start(out_words, y_words[:])
         for q in range(4):

@@ -195,7 +195,7 @@ def tile_picked_zcomp_mul_po_kernel(
             return y_bank[k][:, t, :] if k < 2 else last_banks[t // 2][:, t % 2, :]
 
         y_f32 = [sb("y_f32" + str(k), [P, PACK, pieces[k][2]], F32) for k in range(2)]
-        last_f32 = [sb("last_f32" + str(pair), [P, 2, 64], F32) for pair in range(2)]
+        last_f32 = sb("last_f32", [P, PACK, 64], F32)
         y_bf = [shared[:, base : base + 4 * unit].bitcast(BF16)] + [sb("y_bf" + str(k), [P, 64 * PACK], BF16)[:] for k in (1, 2)]
         y_words = sb("y_words", [P, TARGETS], I32)
         y_scales = sb("y_scales", [P, TARGETS], U8)
@@ -225,22 +225,16 @@ def tile_picked_zcomp_mul_po_kernel(
                     rhs=z_words[u][:, part].bitcast(FP8X4), rhs_scale=z_scales[u][:, part], start=True, stop=True,
                 )
 
-        def round_result(k):
-            nc.scalar.copy(
-                y_bf[k].rearrange("p (v t) -> p v t", t=PACK),
-                y_bank[k].rearrange("p t v -> p v t"),
-            )
-
         def round_fetched(k):
             nc.vector.tensor_copy(
                 y_bf[k].rearrange("p (c i t) -> p c t i", t=PACK, i=4),
                 y_f32[k][:].rearrange("p t (c i) -> p c t i", i=4),
             )
 
-        def fetch_result(k):
+        def fetch_result(k, queue):
             u, lo, n = pieces[k]
             nc.scalar.copy(y_f32[k][:], y_bank[k])
-            nc.sync.dma_start(out_rows[:, :, starts[u] + lo : starts[u] + lo + n], y_f32[k][:])
+            queue.dma_start(out_rows[:, :, starts[u] + lo : starts[u] + lo + n], y_f32[k][:])
 
         def round_pair(pair, copy):
             copy(
@@ -248,9 +242,8 @@ def tile_picked_zcomp_mul_po_kernel(
                 last_banks[pair].rearrange("p t v -> p v t"),
             )
 
-        def fetch_pair(pair, copy, queue):
-            copy(last_f32[pair][:], last_banks[pair])
-            queue.dma_start(out_rows[:, 2 * pair : 2 * pair + 2, :64], last_f32[pair][:])
+        def fetch_pair(pair, copy):
+            copy(last_f32[:, 2 * pair : 2 * pair + 2, :], last_banks[pair])
 
         def quantize_result(k):
             u, lo, n = pieces[k]
@@ -268,20 +261,21 @@ def tile_picked_zcomp_mul_po_kernel(
         last_product(0)
         multiply(1, 1)
         last_product(1)
-        fetch_result(0)
-        fetch_result(1)
-        round_result(1)
+        fetch_result(0, nc.sync)
+        fetch_result(1, nc.scalar)
         multiply(1, 2)
         multiply(1, 3)
         add_messages(2)
         last_product(2)
         round_fetched(0)
-        quantize_result(1)
+        round_fetched(1)
         quantize_result(0)
         round_pair(0, nc.vector.tensor_copy)
         round_pair(1, nc.scalar.copy)
-        fetch_pair(0, nc.vector.tensor_copy, nc.sync)
-        fetch_pair(1, nc.scalar.copy, nc.scalar)
+        quantize_result(1)
+        fetch_pair(0, nc.vector.tensor_copy)
+        fetch_pair(1, nc.scalar.copy)
+        nc.scalar.dma_start(out_rows[:, :, :64], last_f32[:])
         quantize_result(2)
         nc.sync.dma_start(out_words, y_words[:])
         for q in range(4):

@@ -17,7 +17,8 @@ PACK = 4
 TABLE = 1024
 PICKED = 512
 TARGETS = 256
-HALF = 128
+X_FIRST = 4
+W2_FIRST = 8
 FLOPS = 2 * 512 * 512 * (2 * PICKED + TARGETS)
 
 
@@ -49,9 +50,10 @@ def tile_picked_zcomp_mul_po_kernel(
             nc.vector.memset(tile[:].bitcast(I32), 0)
             return tile
 
-        def load_scales(tile, src, queues, quadrants=range(4)):
+        def load_scales(tile, src, queues, quadrants=range(4), first=0):
             for q in quadrants:
-                queues[q % len(queues)].dma_start(tile[32 * q : 32 * q + 4, :].bitcast(I32), src[0, 4 * q : 4 * q + 4, :].bitcast(I32))
+                rows = slice(32 * q + first, 32 * q + first + 4)
+                queues[q % len(queues)].dma_start(tile[rows, :].bitcast(I32), src[0, 4 * q : 4 * q + 4, :].bitcast(I32))
 
         def deal_words(dealt, words, engine):
             engine.tensor_copy(
@@ -83,7 +85,7 @@ def tile_picked_zcomp_mul_po_kernel(
             bank = psum.tile([P, PICKED], F32, name="bank", tag="bank", bufs=5)
             nc.tensor.matmul_mx(
                 out=bank[:], lhsT=w_words[:, cols].bitcast(FP8X4), lhsT_scale=w_scales[:, cols],
-                rhs=words[:].bitcast(FP8X4), rhs_scale=scales[:], start=True, stop=True,
+                rhs=words[:].bitcast(FP8X4), rhs_scale=scales, start=True, stop=True,
             )
             nc.scalar.copy(row, bank[:])
             return row
@@ -95,13 +97,13 @@ def tile_picked_zcomp_mul_po_kernel(
 
         w2_raw = load_words("w2_raw", w2_words)
         attr_sb = load_list("attr_sb", attr)
+        offs_sb = load_list("offs_sb", offs)
         load_scales(e_plane, e_scales, (nc.scalar, nc.sync))
         e_table = load_words("e_table", e_words)
+        load_scales(x_plane, x_scales, (nc.gpsimd,), range(2), X_FIRST)
+        load_scales(w2_plane, w2_scales, (nc.sync,), range(4), W2_FIRST)
+        load_scales(x_plane, x_scales, (nc.sync,), range(2, 4), X_FIRST)
         x_table = load_words("x_table", x_words)
-        load_scales(x_plane, x_scales, (nc.gpsimd,), range(2))
-        load_scales(w2_plane, w2_scales, (nc.sync,))
-        offs_sb = load_list("offs_sb", offs)
-        load_scales(x_plane, x_scales, (nc.sync,), range(2, 4))
         edges = [load_list("edge1_sb", edge1), load_list("edge2_sb", edge2)]
         w1_rows = w1.rearrange("(p j) c -> p j c", j=PACK)
         w1_raw = []
@@ -131,17 +133,17 @@ def tile_picked_zcomp_mul_po_kernel(
         def own_row(name):
             return pool.tile([P, PICKED], F32, name=name, tag=name, align_bytes=64)[:]
 
-        r_rows = [project(own_row("r" + str(t)), t, w2_dealt, w2_dealt_scales, e_picked, e_picked_scales) for t in range(2)]
+        r_rows = [project(own_row("r" + str(t)), t, w2_dealt, w2_dealt_scales[W2_FIRST:, :], e_picked, e_picked_scales[:]) for t in range(2)]
         round_w1(nc.gpsimd.tensor_copy, 0, 0, 128)
         round_w1(nc.scalar.copy, 0, 128, 320)
         round_w1(nc.scalar.copy, 1, 320, 448)
         round_w1(nc.gpsimd.tensor_copy, 1, 448, 512)
         late_rows = pool.tile([P, 2, PICKED], F32, name="late_rows", tag="w1_raw1", align_bytes=64)
         for t in range(2, PACK):
-            r_rows.append(project(late_rows[:, t - 2, :], t, w2_dealt, w2_dealt_scales, e_picked, e_picked_scales))
+            r_rows.append(project(late_rows[:, t - 2, :], t, w2_dealt, w2_dealt_scales[W2_FIRST:, :], e_picked, e_picked_scales[:]))
 
-        x_picked = gather_words("x_picked", x_table, offs_sb)
         x_picked_scales = gather_scales("x_picked_scales", x_plane, offs_sb)
+        x_picked = gather_words("x_picked", x_table, offs_sb)
 
         r_edge = []
 
@@ -157,7 +159,7 @@ def tile_picked_zcomp_mul_po_kernel(
         nc.vector.quantize_mx(
             out=w1_words[:].bitcast(FP8X4), scales=w1_scales[:], in_=w1_bf[:].rearrange("p t m j -> p (t m j)")
         )
-        h_rows = [project(own_row("h" + str(t)), t, w1_words, w1_scales, x_picked, x_picked_scales) for t in range(PACK)]
+        h_rows = [project(own_row("h" + str(t)), t, w1_words, w1_scales[:], x_picked, x_picked_scales[X_FIRST:, :]) for t in range(PACK)]
         unit = 64
         base = 28 * unit
         shared = sb("shared", [P, 48 * unit], F32)

@@ -161,25 +161,25 @@ def tile_picked_zcomp_mul_po_kernel(
         )
         h_rows = [project(own_row("h" + str(t)), t, w1_words, w1_scales[:], x_picked, x_picked_scales[X_FIRST:, :]) for t in range(PACK)]
         unit = 64
-        base = 28 * unit
-        shared = sb("shared", [P, 48 * unit], F32)
+        shared = sb("shared", [P, 60 * unit], F32)
         gather_edges(2, [sb("r_edge2_%d" % d, [P, TARGETS], F32)[:] for d in range(2)])
-        gather_edges(3, [shared[:, base + (4 * d - 1) * unit : base + (4 * d + 3) * unit] for d in range(2)])
+        gather_edges(3, [shared[:, 4 * d * unit : 4 * (d + 1) * unit] for d in range(2)])
         w3_dealt = deal_words(reused.tile([P, 512], I32, name="w3_dealt", align_bytes=64, offset=0), w3_raw, nc.gpsimd)
         w3_dealt_scales = deal_scales(reused.tile([P, 512], U8, name="w3_dealt_scales", align_bytes=64, offset=2048), w3_plane, ((0, 4),))
 
         widths = (192, 64)
         starts = (64, 0)
         pieces = ((0, 64, 128), (0, 0, 64), (1, 0, 64))
-        narrow = shared[:, base : base + 16 * unit].rearrange("p (t v) -> p t v", t=PACK)
+        early = shared[:, : 48 * unit].rearrange("p (t v) -> p t v", t=PACK)
+        late = shared[:, 12 * unit :].rearrange("p (t v) -> p t v", t=PACK)
         messages = [
-            [sb("message0", [P, PACK, 192], F32)[:], shared[:].rearrange("p (t v) -> p t v", t=PACK)[:, :, :192]],
-            [narrow[:, :, unit * d : unit * (d + 1)] for d in range(2)],
+            [sb("message0", [P, PACK, 192], F32)[:], late[:, :, :192]],
+            [early[:, :, unit : 2 * unit], late[:, :, :unit]],
         ]
 
-        def multiply(u, t):
+        def multiply(u, t, sides=range(2)):
             lo, hi = starts[u], starts[u] + widths[u]
-            for d in range(2):
+            for d in sides:
                 nc.vector.tensor_tensor(
                     messages[u][d][:, t, :],
                     h_rows[t].indirect(places[d][:, lo // 16 : hi // 16]),
@@ -187,18 +187,19 @@ def tile_picked_zcomp_mul_po_kernel(
                     MULT,
                 )
 
-        z_bf = [shared[:, base + 12 * unit : base + 18 * unit].bitcast(BF16), sb("z_bf", [P, 64 * PACK], BF16)[:]]
+        z_bf = [sb("z_wide", [P, 192 * PACK], BF16)[:], sb("z_bf", [P, 64 * PACK], BF16)[:]]
         z_words = [sb("z_words" + str(u), [P, widths[u]], U32) for u in range(2)]
         z_scales = [sb("z_scales" + str(u), [P, widths[u]], U8) for u in range(2)]
-        y_bank = [psum.tile([P, PACK, n], F32, name="y_bank%d_%d" % (u, lo))[:] for u, lo, n in pieces[:2]]
+        first_banks = [psum.tile([P, 2, 128], F32, name="first_bank" + str(pair))[:] for pair in range(2)]
+        second_bank = psum.tile([P, PACK, 64], F32, name="second_bank")[:]
         last_banks = [psum.tile([P, 2, 64], F32, name="last_bank" + str(pair), tag="bank", bufs=5)[:] for pair in range(2)]
 
         def result_rows(k, t):
-            return y_bank[k][:, t, :] if k < 2 else last_banks[t // 2][:, t % 2, :]
+            return second_bank[:, t, :] if k == 1 else (first_banks, None, last_banks)[k][t // 2][:, t % 2, :]
 
         y_f32 = [sb("y_f32" + str(k), [P, PACK, pieces[k][2]], F32) for k in range(2)]
         last_f32 = sb("last_f32", [P, PACK, 64], F32)
-        y_bf = [shared[:, base : base + 4 * unit].bitcast(BF16)] + [sb("y_bf" + str(k), [P, 64 * PACK], BF16)[:] for k in (1, 2)]
+        y_bf = [shared[:, 12 * unit : 16 * unit].bitcast(BF16)] + [sb("y_bf" + str(k), [P, 64 * PACK], BF16)[:] for k in (1, 2)]
         y_words = sb("y_words", [P, TARGETS], I32)
         y_scales = sb("y_scales", [P, TARGETS], U8)
         out_rows = out_0.rearrange("(p t) v -> p t v", t=PACK)
@@ -235,7 +236,11 @@ def tile_picked_zcomp_mul_po_kernel(
 
         def fetch_result(k, queue):
             u, lo, n = pieces[k]
-            nc.scalar.copy(y_f32[k][:], y_bank[k])
+            if k == 0:
+                for pair in range(2):
+                    nc.scalar.copy(y_f32[k][:, 2 * pair : 2 * pair + 2, :], first_banks[pair])
+            else:
+                nc.scalar.copy(y_f32[k][:], second_bank)
             queue.dma_start(out_rows[:, :, starts[u] + lo : starts[u] + lo + n], y_f32[k][:])
 
         def round_pair(pair, copy):
@@ -257,14 +262,15 @@ def tile_picked_zcomp_mul_po_kernel(
 
         for t in range(PACK):
             multiply(0, t)
-        multiply(1, 0)
+        multiply(1, 0, (0,))
         add_messages(0)
         add_messages(1)
         last_product(0)
-        multiply(1, 1)
         last_product(1)
         fetch_result(0, nc.sync)
         fetch_result(1, nc.scalar)
+        multiply(1, 0, (1,))
+        multiply(1, 1)
         multiply(1, 2)
         multiply(1, 3)
         add_messages(2)

@@ -278,6 +278,7 @@ def tile_picked_zcomp_mul_po_kernel(
         round_fetched(0)
         round_fetched(1)
         quantize_result(0)
+        nc.sync.dma_start(out_words[:, 128:], y_words[:, 128:])
         round_pair(0, nc.vector.tensor_copy)
         round_pair(1, nc.scalar.copy)
         quantize_result(1)
@@ -285,7 +286,7 @@ def tile_picked_zcomp_mul_po_kernel(
         fetch_pair(1, nc.scalar.copy)
         nc.scalar.dma_start(out_rows[:, :, :64], last_f32[:])
         quantize_result(2)
-        nc.sync.dma_start(out_words, y_words[:])
+        nc.sync.dma_start(out_words[:, :128], y_words[:, :128])
         for q in range(4):
             queue = nc.sync if q % 2 else nc.scalar
             queue.dma_start(out_2[0, 4 * q : 4 * q + 4, :].bitcast(I32), y_scales[32 * q : 32 * q + 4, :].bitcast(I32))

@@ -199,7 +199,7 @@ def tile_picked_zcomp_mul_po_kernel(
 
         y_f32 = [sb("y_f32" + str(k), [P, PACK, pieces[k][2]], F32) for k in range(2)]
         last_f32 = sb("last_f32", [P, PACK, 64], F32)
-        y_bf = [shared[:, 12 * unit : 16 * unit].bitcast(BF16)] + [sb("y_bf" + str(k), [P, 64 * PACK], BF16)[:] for k in (1, 2)]
+        y_bf = [shared[:, 12 * unit : 16 * unit].bitcast(BF16), shared[:, 24 * unit : 26 * unit].bitcast(BF16), sb("y_bf2", [P, 64 * PACK], BF16)[:]]
         y_words = sb("y_words", [P, TARGETS], I32)
         y_scales = sb("y_scales", [P, TARGETS], U8)
         out_rows = out_0.rearrange("(p t) v -> p t v", t=PACK)
@@ -263,30 +263,30 @@ def tile_picked_zcomp_mul_po_kernel(
         for t in range(PACK):
             multiply(0, t)
         multiply(1, 0, (0,))
-        add_messages(0)
         add_messages(1)
-        last_product(0)
+        add_messages(0)
         last_product(1)
-        fetch_result(0, nc.sync)
-        fetch_result(1, nc.scalar)
         multiply(1, 0, (1,))
+        last_product(0)
+        fetch_result(1, nc.sync)
+        fetch_result(0, nc.scalar)
         multiply(1, 1)
         multiply(1, 2)
         multiply(1, 3)
         add_messages(2)
         last_product(2)
-        round_fetched(0)
         round_fetched(1)
+        round_fetched(0)
+        quantize_result(1)
         quantize_result(0)
-        nc.sync.dma_start(out_words[:, 128:], y_words[:, 128:])
+        nc.sync.dma_start(out_words[:, 64:], y_words[:, 64:])
         round_pair(0, nc.vector.tensor_copy)
         round_pair(1, nc.scalar.copy)
-        quantize_result(1)
         fetch_pair(0, nc.vector.tensor_copy)
         fetch_pair(1, nc.scalar.copy)
         nc.scalar.dma_start(out_rows[:, :, :64], last_f32[:])
         quantize_result(2)
-        nc.sync.dma_start(out_words[:, :128], y_words[:, :128])
+        nc.sync.dma_start(out_words[:, :64], y_words[:, :64])
         for q in range(4):
             queue = nc.sync if q % 2 else nc.scalar
             queue.dma_start(out_2[0, 4 * q : 4 * q + 4, :].bitcast(I32), y_scales[32 * q : 32 * q + 4, :].bitcast(I32))

@@ -160,22 +160,23 @@ def tile_picked_zcomp_mul_po_kernel(
             out=w1_words[:].bitcast(FP8X4), scales=w1_scales[:], in_=w1_bf[:].rearrange("p t m j -> p (t m j)")
         )
         h_rows = [project(own_row("h" + str(t)), t, w1_words, w1_scales[:], x_picked, x_picked_scales[X_FIRST:, :]) for t in range(PACK)]
-        unit = 64
-        shared = sb("shared", [P, 60 * unit], F32)
+        room = [sb("room0", [P, 1856], F32), sb("room1", [P, 832], F32)]
         gather_edges(2, [sb("r_edge2_%d" % d, [P, TARGETS], F32)[:] for d in range(2)])
-        gather_edges(3, [shared[:, 4 * d * unit : 4 * (d + 1) * unit] for d in range(2)])
+        gather_edges(3, [room[0][:, 256:512], sb("r_edge3_1", [P, TARGETS], F32)[:]])
         w3_dealt = deal_words(reused.tile([P, 512], I32, name="w3_dealt", align_bytes=64, offset=0), w3_raw, nc.gpsimd)
         w3_dealt_scales = deal_scales(reused.tile([P, 512], U8, name="w3_dealt_scales", align_bytes=64, offset=2048), w3_plane, ((0, 4),))
 
         widths = (192, 64)
         starts = (64, 0)
         pieces = ((0, 64, 128), (0, 0, 64), (1, 0, 64))
-        early = shared[:, : 48 * unit].rearrange("p (t v) -> p t v", t=PACK)
-        late = shared[:, 12 * unit :].rearrange("p (t v) -> p t v", t=PACK)
         messages = [
-            [sb("message0", [P, PACK, 192], F32)[:], late[:, :, :192]],
-            [early[:, :, unit : 2 * unit], late[:, :, :unit]],
+            [room[d][:, 64:].rearrange("p (t v) -> p t v", t=PACK)[:, :, :192] for d in range(2)],
+            [room[d][:, :end].rearrange("p (t v) -> p t v", t=PACK)[:, :, :64] for d, end in enumerate((1280, 768))],
         ]
+
+        def multiply_whole():
+            for d in range(2):
+                nc.vector.tensor_tensor(room[d][:, :TARGETS], h_rows[0].indirect(places[d][:]), r_edge[0][d], MULT)
 
         def multiply(u, t, sides=range(2)):
             lo, hi = starts[u], starts[u] + widths[u]
@@ -199,7 +200,7 @@ def tile_picked_zcomp_mul_po_kernel(
 
         y_f32 = [sb("y_f32" + str(k), [P, PACK, pieces[k][2]], F32) for k in range(2)]
         last_f32 = sb("last_f32", [P, PACK, 64], F32)
-        y_bf = [shared[:, 12 * unit : 16 * unit].bitcast(BF16), shared[:, 24 * unit : 26 * unit].bitcast(BF16), sb("y_bf2", [P, 64 * PACK], BF16)[:]]
+        y_bf = [room[1][:, :256].bitcast(BF16), room[0][:, :128].bitcast(BF16), sb("y_bf2", [P, 64 * PACK], BF16)[:]]
         y_words = sb("y_words", [P, TARGETS], I32)
         y_scales = sb("y_scales", [P, TARGETS], U8)
         out_rows = out_0.rearrange("(p t) v -> p t v", t=PACK)
@@ -260,19 +261,20 @@ def tile_picked_zcomp_mul_po_kernel(
                 in_=y_bf[k],
             )
 
-        for t in range(PACK):
+        multiply_whole()
+        for t in range(1, PACK):
             multiply(0, t)
-        multiply(1, 0, (0,))
+        multiply(1, 1, (0,))
         add_messages(1)
         add_messages(0)
         last_product(1)
-        multiply(1, 0, (1,))
+        multiply(1, 3, (0,))
         last_product(0)
         fetch_result(1, nc.sync)
         fetch_result(0, nc.scalar)
-        multiply(1, 1)
+        multiply(1, 1, (1,))
         multiply(1, 2)
-        multiply(1, 3)
+        multiply(1, 3, (1,))
         add_messages(2)
         last_product(2)
         round_fetched(1)
@@ -280,13 +282,13 @@ def tile_picked_zcomp_mul_po_kernel(
         quantize_result(1)
         quantize_result(0)
         nc.sync.dma_start(out_words[:, 64:], y_words[:, 64:])
+        fetch_pair(0, nc.scalar.copy)
+        fetch_pair(1, nc.scalar.copy)
+        nc.sync.dma_start(out_rows[:, :, :64], last_f32[:])
         round_pair(0, nc.vector.tensor_copy)
         round_pair(1, nc.scalar.copy)
-        fetch_pair(0, nc.vector.tensor_copy)
-        fetch_pair(1, nc.scalar.copy)
-        nc.scalar.dma_start(out_rows[:, :, :64], last_f32[:])
         quantize_result(2)
-        nc.sync.dma_start(out_words[:, :64], y_words[:, :64])
+        nc.scalar.dma_start(out_words[:, :64], y_words[:, :64])
         for q in range(4):
-            queue = nc.sync if q % 2 else nc.scalar
+            queue = nc.sync if q else nc.scalar
             queue.dma_start(out_2[0, 4 * q : 4 * q + 4, :].bitcast(I32), y_scales[32 * q : 32 * q + 4, :].bitcast(I32))

@@ -11,6 +11,7 @@ U8 = mybir.dt.uint8
 FP8X4 = mybir.dt.float8_e4m3fn_x4
 MULT = mybir.AluOpType.mult
 ADD = mybir.AluOpType.add
+COPY = mybir.ActivationFunctionType.Copy
 
 P = 128
 PACK = 4
@@ -55,14 +56,16 @@ def tile_picked_zcomp_mul_po_kernel(
                 rows = slice(32 * q + first, 32 * q + first + 4)
                 queues[q % len(queues)].dma_start(tile[rows, :].bitcast(I32), src[0, 4 * q : 4 * q + 4, :].bitcast(I32))
 
-        def deal_words(dealt, words, engine):
-            engine.tensor_copy(
+        def deal_words(name, words):
+            dealt = sb(name, [P, 512], I32)
+            nc.gpsimd.tensor_copy(
                 dealt[:].rearrange("p (t c i) -> p c t i", t=PACK, i=4),
                 words[:].rearrange("p (c i t) -> p c t i", t=PACK, i=4),
             )
             return dealt
 
-        def deal_scales(dealt, scales, cuts):
+        def deal_scales(name, scales, cuts):
+            dealt = sb(name, [P, 512], U8)
             for lo, hi in cuts:
                 nc.gpsimd.tensor_copy(
                     dealt[:].rearrange("p (t m) -> p t m", t=PACK)[:, lo:hi, :],
@@ -75,20 +78,19 @@ def tile_picked_zcomp_mul_po_kernel(
             nc.vector.tensor_copy(picked[:], words[:].bitcast(U32).indirect(offsets[:]))
             return picked
 
-        def gather_scales(name, scales, offsets, tag=None):
-            picked = sb(name, [P, PICKED], U8, tag)
+        def gather_scales(name, scales, offsets):
+            picked = sb(name, [P, PICKED], U8)
             nc.vector.tensor_copy(picked[:], scales[:].indirect(offsets[:]))
             return picked
 
-        def project(row, t, w_words, w_scales, words, scales):
+        def project(name, t, w_words, w_scales, words, scales):
             cols = slice(t * P, (t + 1) * P)
-            bank = psum.tile([P, PICKED], F32, name="bank", tag="bank", bufs=5)
+            bank = psum.tile([P, PICKED], F32, name=name, tag="bank", bufs=8)
             nc.tensor.matmul_mx(
                 out=bank[:], lhsT=w_words[:, cols].bitcast(FP8X4), lhsT_scale=w_scales[:, cols],
                 rhs=words[:].bitcast(FP8X4), rhs_scale=scales, start=True, stop=True,
             )
-            nc.scalar.copy(row, bank[:])
-            return row
+            return bank
 
         e_plane = cleared_plane("e_plane", TABLE)
         x_plane = cleared_plane("x_plane", TABLE)
@@ -104,24 +106,33 @@ def tile_picked_zcomp_mul_po_kernel(
         load_scales(w2_plane, w2_scales, (nc.sync,), range(4), W2_FIRST)
         load_scales(x_plane, x_scales, (nc.sync,), range(2, 4), X_FIRST)
         x_table = load_words("x_table", x_words)
-        edges = [load_list("edge1_sb", edge1), load_list("edge2_sb", edge2)]
         w1_rows = w1.rearrange("(p j) c -> p j c", j=PACK)
-        w1_raw = []
         w1_cuts = ((0, 320), (320, 512))
+        w1_raw = []
         for u, (lo, hi) in enumerate(w1_cuts):
-            part = pool.tile([P, PACK, hi - lo], F32, name="w1_raw" + str(u), tag="w1_raw" + str(u), align_bytes=64)
+            part = sb("w1_raw" + str(u), [P, PACK, hi - lo], F32)
             nc.sync.dma_start(part[:], w1_rows[:, :, lo:hi])
             w1_raw.append(part)
+        edges = [load_list("edge1_sb", edge1), load_list("edge2_sb", edge2)]
         places = [load_list("pos1_sb", pos1), load_list("pos2_sb", pos2)]
         w3_raw = load_words("w3_raw", w3_words)
         load_scales(w3_plane, w3_scales, (nc.sync,))
 
-        w2_dealt = deal_words(sb("w2_dealt", [P, 512], I32), w2_raw, nc.gpsimd)
+        w2_dealt = deal_words("w2_dealt", w2_raw)
         e_picked_scales = gather_scales("e_picked_scales", e_plane, attr_sb)
         e_picked = gather_words("e_picked", e_table, attr_sb)
-        w2_dealt_scales = deal_scales(sb("w2_dealt_scales", [P, 512], U8), w2_plane, ((0, 2), (2, 4)))
+        w2_dealt_scales = deal_scales("w2_dealt_scales", w2_plane, ((0, 2), (2, 4)))
+        r_banks = [
+            project("r_bank", t, w2_dealt, w2_dealt_scales[W2_FIRST:, :], e_picked, e_picked_scales[:])
+            for t in range(PACK)
+        ]
+        x_picked_scales = gather_scales("x_picked_scales", x_plane, offs_sb)
+        x_picked = gather_words("x_picked", x_table, offs_sb)
 
-        w1_bf = reused.tile([P, PACK, P, PACK], BF16, name="w1_bf", align_bytes=64, offset=0)
+        def shared(name, shape, dtype, offset):
+            return reused.tile(shape, dtype, name=name, align_bytes=64, offset=offset)
+
+        w1_bf = shared("w1_bf", [P, PACK, P, PACK], BF16, 0)
 
         def round_w1(copy, u, lo, hi):
             first = w1_cuts[u][0]
@@ -130,165 +141,142 @@ def tile_picked_zcomp_mul_po_kernel(
                 w1_raw[u][:, :, lo - first : hi - first].rearrange("p j (m t) -> p m t j", t=PACK),
             )
 
-        def own_row(name):
-            return pool.tile([P, PICKED], F32, name=name, tag=name, align_bytes=64)[:]
-
-        r_rows = [project(own_row("r" + str(t)), t, w2_dealt, w2_dealt_scales[W2_FIRST:, :], e_picked, e_picked_scales[:]) for t in range(2)]
-        round_w1(nc.gpsimd.tensor_copy, 0, 0, 128)
-        round_w1(nc.scalar.copy, 0, 128, 320)
-        round_w1(nc.scalar.copy, 1, 320, 448)
-        round_w1(nc.gpsimd.tensor_copy, 1, 448, 512)
-        late_rows = pool.tile([P, 2, PICKED], F32, name="late_rows", tag="w1_raw1", align_bytes=64)
-        for t in range(2, PACK):
-            r_rows.append(project(late_rows[:, t - 2, :], t, w2_dealt, w2_dealt_scales[W2_FIRST:, :], e_picked, e_picked_scales[:]))
-
-        x_picked_scales = gather_scales("x_picked_scales", x_plane, offs_sb)
-        x_picked = gather_words("x_picked", x_table, offs_sb)
-
-        r_edge = []
-
-        def gather_edges(t, rooms):
-            for d in range(2):
-                nc.vector.tensor_copy(rooms[d], r_rows[t].indirect(edges[d][:]))
-            r_edge.append(rooms)
-
-        for t in range(2):
-            gather_edges(t, [sb("r_edge%d_%d" % (t, d), [P, TARGETS], F32)[:] for d in range(2)])
-        w1_words = pool.tile([P, 512], U32, name="w1_words", align_bytes=64)
-        w1_scales = sb("w1_scales", [P, 512], U8)
-        nc.vector.quantize_mx(
-            out=w1_words[:].bitcast(FP8X4), scales=w1_scales[:], in_=w1_bf[:].rearrange("p t m j -> p (t m j)")
-        )
-        h_rows = [project(own_row("h" + str(t)), t, w1_words, w1_scales[:], x_picked, x_picked_scales[X_FIRST:, :]) for t in range(PACK)]
-        room = [sb("room0", [P, 1856], F32), sb("room1", [P, 832], F32)]
-        gather_edges(2, [sb("r_edge2_%d" % d, [P, TARGETS], F32)[:] for d in range(2)])
-        gather_edges(3, [room[0][:, 256:512], sb("r_edge3_1", [P, TARGETS], F32)[:]])
-        w3_dealt = deal_words(reused.tile([P, 512], I32, name="w3_dealt", align_bytes=64, offset=0), w3_raw, nc.gpsimd)
-        w3_dealt_scales = deal_scales(reused.tile([P, 512], U8, name="w3_dealt_scales", align_bytes=64, offset=2048), w3_plane, ((0, 4),))
-
-        widths = (192, 64)
-        starts = (64, 0)
-        pieces = ((0, 64, 128), (0, 0, 64), (1, 0, 64))
-        messages = [
-            [room[d][:, 64:].rearrange("p (t v) -> p t v", t=PACK)[:, :, :192] for d in range(2)],
-            [room[d][:, :end].rearrange("p (t v) -> p t v", t=PACK)[:, :, :64] for d, end in enumerate((1280, 768))],
+        round_w1(nc.gpsimd.tensor_copy, 0, 0, 160)
+        round_w1(nc.vector.tensor_copy, 0, 160, 320)
+        round_w1(nc.vector.tensor_copy, 1, 320, 512)
+        w1_flat = w1_bf[:].rearrange("p t m j -> p (t m j)")
+        w1_words = [shared("w1_words0", [P, P], U32, 4096), sb("w1_words1", [P, 3 * P], U32)]
+        w1_scales = [sb("w1_scales0", [P, P], U8), sb("w1_scales1", [P, 3 * P], U8)]
+        nc.vector.quantize_mx(out=w1_words[0][:].bitcast(FP8X4), scales=w1_scales[0][:], in_=w1_flat[:, :512])
+        nc.vector.quantize_mx(out=w1_words[1][:].bitcast(FP8X4), scales=w1_scales[1][:], in_=w1_flat[:, 512:])
+        first_halves = []
+        for half in range(2):
+            cols = slice(half * 256, (half + 1) * 256)
+            bank = psum.tile([P, 256], F32, name="h_half", tag="bank", bufs=8)
+            nc.tensor.matmul_mx(
+                out=bank[:], lhsT=w1_words[0][:].bitcast(FP8X4), lhsT_scale=w1_scales[0][:],
+                rhs=x_picked[:, cols].bitcast(FP8X4), rhs_scale=x_picked_scales[X_FIRST:, cols], start=True, stop=True,
+            )
+            first_halves.append(bank)
+        h_banks = [None] + [
+            project("h_bank", t, w1_words[1], w1_scales[1][:], x_picked, x_picked_scales[X_FIRST:, :]) for t in range(PACK - 1)
         ]
+        w3_dealt = deal_words("w3_dealt", w3_raw)
+        w3_dealt_scales = deal_scales("w3_dealt_scales", w3_plane, ((0, 4),))
 
-        def multiply_whole():
-            for d in range(2):
-                nc.vector.tensor_tensor(room[d][:, :TARGETS], h_rows[0].indirect(places[d][:]), r_edge[0][d], MULT)
+        def fetch(name, copy, bank):
+            row = sb(name, [P, PICKED], F32)
+            copy(row[:], bank[:])
+            return row
 
-        def multiply(u, t, sides=range(2)):
-            lo, hi = starts[u], starts[u] + widths[u]
+        picked_edges = [[None, None] for t in range(PACK)]
+        messages = [sb("messages" + str(d), [P, PACK, TARGETS], F32) for d in range(2)]
+        r_rows = [fetch("r" + str(t), nc.scalar.copy, r_banks[t]) for t in range(PACK)]
+        h_rows = [None] * PACK
+
+        def gather_edges_scalar(t, d, offset):
+            picked_edges[t][d] = shared("picked_edges%d_%d" % (t, d), [P, TARGETS], F32, offset)
+            nc.scalar.activation(picked_edges[t][d][:], r_rows[t][:].indirect(edges[d][:]), COPY)
+
+        def gather_edges_vector(t, d, offset):
+            picked_edges[t][d] = shared("picked_edges%d_%d" % (t, d), [P, TARGETS], F32, offset)
+            nc.vector.tensor_copy(picked_edges[t][d][:], r_rows[t][:].indirect(edges[d][:]))
+
+        def fetch_nodes(t):
+            h_rows[t] = fetch("h" + str(t), nc.scalar.copy, h_banks[t])
+
+        def multiply(t, lo, hi, sides=range(2)):
             for d in sides:
                 nc.vector.tensor_tensor(
-                    messages[u][d][:, t, :],
-                    h_rows[t].indirect(places[d][:, lo // 16 : hi // 16]),
-                    r_edge[t][d][:, lo:hi],
-                    MULT,
+                    messages[d][:, t, lo:hi], h_rows[t][:].indirect(places[d][:, lo // 16 : hi // 16]),
+                    picked_edges[t][d][:, lo:hi], MULT,
                 )
 
-        z_bf = [sb("z_wide", [P, 192 * PACK], BF16)[:], sb("z_bf", [P, 64 * PACK], BF16)[:]]
-        z_words = [sb("z_words" + str(u), [P, widths[u]], U32) for u in range(2)]
-        z_scales = [sb("z_scales" + str(u), [P, widths[u]], U8) for u in range(2)]
-        first_banks = [psum.tile([P, 2, 128], F32, name="first_bank" + str(pair))[:] for pair in range(2)]
-        second_bank = psum.tile([P, PACK, 64], F32, name="second_bank")[:]
-        last_banks = [psum.tile([P, 2, 64], F32, name="last_bank" + str(pair), tag="bank", bufs=5)[:] for pair in range(2)]
-
-        def result_rows(k, t):
-            return second_bank[:, t, :] if k == 1 else (first_banks, None, last_banks)[k][t // 2][:, t % 2, :]
-
-        y_f32 = [sb("y_f32" + str(k), [P, PACK, pieces[k][2]], F32) for k in range(2)]
-        last_f32 = sb("last_f32", [P, PACK, 64], F32)
-        y_bf = [room[1][:, :256].bitcast(BF16), room[0][:, :128].bitcast(BF16), sb("y_bf2", [P, 64 * PACK], BF16)[:]]
+        pieces = ((0, 128), (128, 192), (192, 256))
+        z_bf = [sb("z_bf" + str(k), [P, (hi - lo) * PACK], BF16) for k, (lo, hi) in enumerate(pieces)]
+        z_words = [sb("z_words" + str(k), [P, hi - lo], U32) for k, (lo, hi) in enumerate(pieces)]
+        z_scales = [sb("z_scales" + str(k), [P, hi - lo], U8) for k, (lo, hi) in enumerate(pieces)]
+        y_f32 = [sb("y_f32" + str(k), [P, PACK, hi - lo], F32) for k, (lo, hi) in enumerate(pieces)]
+        y_bf = [sb("y_bf" + str(k), [P, hi - lo, PACK], BF16) for k, (lo, hi) in enumerate(pieces)]
         y_words = sb("y_words", [P, TARGETS], I32)
         y_scales = sb("y_scales", [P, TARGETS], U8)
         out_rows = out_0.rearrange("(p t) v -> p t v", t=PACK)
         out_words = out_1[0].rearrange("p v t -> p (v t)").bitcast(I32)
 
         def add_messages(k):
-            u, lo, n = pieces[k]
+            lo, hi = pieces[k]
             nc.vector.tensor_tensor(
-                z_bf[u][:, PACK * lo : PACK * (lo + n)].rearrange("p (c i t) -> p c t i", t=PACK, i=4),
-                messages[u][0][:, :, lo : lo + n].rearrange("p t (c i) -> p c t i", i=4),
-                messages[u][1][:, :, lo : lo + n].rearrange("p t (c i) -> p c t i", i=4),
+                z_bf[k][:].rearrange("p (c i t) -> p c t i", t=PACK, i=4),
+                messages[0][:, :, lo:hi].rearrange("p t (c i) -> p c t i", i=4),
+                messages[1][:, :, lo:hi].rearrange("p t (c i) -> p c t i", i=4),
                 ADD,
             )
 
         def last_product(k):
-            u, lo, n = pieces[k]
-            part = slice(lo, lo + n)
-            nc.vector.quantize_mx(
-                out=z_words[u][:, part].bitcast(FP8X4), scales=z_scales[u][:, part],
-                in_=z_bf[u][:, PACK * lo : PACK * (lo + n)],
-            )
+            lo, hi = pieces[k]
+            nc.vector.quantize_mx(out=z_words[k][:].bitcast(FP8X4), scales=z_scales[k][:], in_=z_bf[k][:])
+            banks = [psum.tile([P, 2, hi - lo], F32, name="y_bank", tag="bank", bufs=8) for pair in range(2)]
             for t in range(PACK):
                 cols = slice(t * P, (t + 1) * P)
                 nc.tensor.matmul_mx(
-                    out=result_rows(k, t), lhsT=w3_dealt[:, cols].bitcast(FP8X4), lhsT_scale=w3_dealt_scales[:, cols],
-                    rhs=z_words[u][:, part].bitcast(FP8X4), rhs_scale=z_scales[u][:, part], start=True, stop=True,
+                    out=banks[t // 2][:, t % 2, :], lhsT=w3_dealt[:, cols].bitcast(FP8X4), lhsT_scale=w3_dealt_scales[:, cols],
+                    rhs=z_words[k][:].bitcast(FP8X4), rhs_scale=z_scales[k][:], start=True, stop=True,
                 )
+            return banks
 
-        def round_fetched(k):
-            nc.vector.tensor_copy(
-                y_bf[k].rearrange("p (c i t) -> p c t i", t=PACK, i=4),
-                y_f32[k][:].rearrange("p t (c i) -> p c t i", i=4),
-            )
+        def fetch_result(k, banks, queue):
+            lo, hi = pieces[k]
+            for pair in range(2):
+                nc.scalar.copy(y_f32[k][:, 2 * pair : 2 * pair + 2, :], banks[pair][:])
+            queue.dma_start(out_rows[:, :, lo:hi], y_f32[k][:])
 
-        def fetch_result(k, queue):
-            u, lo, n = pieces[k]
-            if k == 0:
-                for pair in range(2):
-                    nc.scalar.copy(y_f32[k][:, 2 * pair : 2 * pair + 2, :], first_banks[pair])
-            else:
-                nc.scalar.copy(y_f32[k][:], second_bank)
-            queue.dma_start(out_rows[:, :, starts[u] + lo : starts[u] + lo + n], y_f32[k][:])
-
-        def round_pair(pair, copy):
-            copy(
-                y_bf[2].rearrange("p (v t) -> p v t", t=PACK)[:, :, 2 * pair : 2 * pair + 2],
-                last_banks[pair].rearrange("p t v -> p v t"),
-            )
-
-        def fetch_pair(pair, copy):
-            copy(last_f32[:, 2 * pair : 2 * pair + 2, :], last_banks[pair])
+        def round_result(k, banks, copy):
+            for pair in range(2):
+                copy(y_bf[k][:, :, 2 * pair : 2 * pair + 2], banks[pair][:].rearrange("p t v -> p v t"))
 
         def quantize_result(k):
-            u, lo, n = pieces[k]
+            lo, hi = pieces[k]
             nc.vector.quantize_mx(
-                out=y_words[:, starts[u] + lo : starts[u] + lo + n].bitcast(FP8X4),
-                scales=y_scales[:, starts[u] + lo : starts[u] + lo + n],
-                in_=y_bf[k],
+                out=y_words[:, lo:hi].bitcast(FP8X4), scales=y_scales[:, lo:hi], in_=y_bf[k][:].rearrange("p v t -> p (v t)")
             )
 
-        multiply_whole()
-        for t in range(1, PACK):
-            multiply(0, t)
-        multiply(1, 1, (0,))
-        add_messages(1)
+        gather_edges_scalar(0, 0, 8192)
+        gather_edges_scalar(0, 1, 9216)
+        gather_edges_vector(1, 0, 1024)
+        h_rows[0] = sb("h0", [P, PICKED], F32)
+        for half in range(2):
+            nc.scalar.copy(h_rows[0][:, half * 256 : (half + 1) * 256], first_halves[half][:])
+        fetch_nodes(1)
+        gather_edges_scalar(1, 1, 4096)
+        multiply(0, 0, TARGETS)
+        gather_edges_scalar(2, 0, 8192)
+        fetch_nodes(2)
+        gather_edges_scalar(2, 1, 9216)
+        multiply(1, 0, TARGETS)
+        gather_edges_scalar(3, 0, 1024)
+        fetch_nodes(3)
+        gather_edges_scalar(3, 1, 4096)
+        multiply(2, 0, TARGETS)
+        multiply(3, *pieces[0])
+        multiply(3, *pieces[1])
         add_messages(0)
-        last_product(1)
-        multiply(1, 3, (0,))
-        last_product(0)
-        fetch_result(1, nc.sync)
-        fetch_result(0, nc.scalar)
-        multiply(1, 1, (1,))
-        multiply(1, 2)
-        multiply(1, 3, (1,))
+        add_messages(1)
+        banks0 = last_product(0)
+        multiply(3, *pieces[2])
+        banks1 = last_product(1)
         add_messages(2)
-        last_product(2)
-        round_fetched(1)
-        round_fetched(0)
-        quantize_result(1)
+        banks2 = last_product(2)
+        fetch_result(0, banks0, nc.scalar)
+        round_result(0, banks0, nc.scalar.copy)
+        fetch_result(1, banks1, nc.sync)
+        round_result(1, banks1, nc.vector.tensor_copy)
         quantize_result(0)
-        nc.sync.dma_start(out_words[:, 64:], y_words[:, 64:])
-        fetch_pair(0, nc.scalar.copy)
-        fetch_pair(1, nc.scalar.copy)
-        nc.sync.dma_start(out_rows[:, :, :64], last_f32[:])
-        round_pair(0, nc.vector.tensor_copy)
-        round_pair(1, nc.scalar.copy)
+        quantize_result(1)
+        nc.sync.dma_start(out_words[:, :192], y_words[:, :192])
+        fetch_result(2, banks2, nc.sync)
+        round_result(2, banks2, nc.vector.tensor_copy)
         quantize_result(2)
-        nc.scalar.dma_start(out_words[:, :64], y_words[:, :64])
+        nc.scalar.dma_start(out_words[:, 192:], y_words[:, 192:])
         for q in range(4):
             queue = nc.sync if q else nc.scalar
             queue.dma_start(out_2[0, 4 * q : 4 * q + 4, :].bitcast(I32), y_scales[32 * q : 32 * q + 4, :].bitcast(I32))

@@ -56,18 +56,16 @@ def tile_picked_zcomp_mul_po_kernel(
                 rows = slice(32 * q + first, 32 * q + first + 4)
                 queues[q % len(queues)].dma_start(tile[rows, :].bitcast(I32), src[0, 4 * q : 4 * q + 4, :].bitcast(I32))
 
-        def deal_words(name, words):
-            dealt = sb(name, [P, 512], I32)
-            nc.gpsimd.tensor_copy(
+        def deal_words(dealt, words, copy):
+            copy(
                 dealt[:].rearrange("p (t c i) -> p c t i", t=PACK, i=4),
-                words[:].rearrange("p (c i t) -> p c t i", t=PACK, i=4),
+                words.rearrange("p (c i t) -> p c t i", t=PACK, i=4),
             )
             return dealt
 
-        def deal_scales(name, scales, cuts):
-            dealt = sb(name, [P, 512], U8)
+        def deal_scales(dealt, scales, cuts, engine):
             for lo, hi in cuts:
-                nc.gpsimd.tensor_copy(
+                engine.tensor_copy(
                     dealt[:].rearrange("p (t m) -> p t m", t=PACK)[:, lo:hi, :],
                     scales[:].rearrange("p (m t) -> p t m", t=PACK)[:, lo:hi, :],
                 )
@@ -96,15 +94,15 @@ def tile_picked_zcomp_mul_po_kernel(
         x_plane = cleared_plane("x_plane", TABLE)
         w2_plane = cleared_plane("w2_plane", 512)
         w3_plane = cleared_plane("w3_plane", 512)
+        x_picked_scales = cleared_plane("x_picked_scales", PICKED)
 
         w2_raw = load_words("w2_raw", w2_words)
         attr_sb = load_list("attr_sb", attr)
         offs_sb = load_list("offs_sb", offs)
         load_scales(e_plane, e_scales, (nc.scalar, nc.sync))
         e_table = load_words("e_table", e_words)
-        load_scales(x_plane, x_scales, (nc.gpsimd,), range(2), X_FIRST)
         load_scales(w2_plane, w2_scales, (nc.sync,), range(4), W2_FIRST)
-        load_scales(x_plane, x_scales, (nc.sync,), range(2, 4), X_FIRST)
+        nc.sync.dma_start(x_plane[:16, :].bitcast(I32), x_scales[0].bitcast(I32))
         x_table = load_words("x_table", x_words)
         w1_rows = w1.rearrange("(p j) c -> p j c", j=PACK)
         w1_cuts = ((0, 320), (320, 512))
@@ -114,19 +112,24 @@ def tile_picked_zcomp_mul_po_kernel(
             nc.sync.dma_start(part[:], w1_rows[:, :, lo:hi])
             w1_raw.append(part)
         edges = [load_list("edge1_sb", edge1), load_list("edge2_sb", edge2)]
-        places = [load_list("pos1_sb", pos1), load_list("pos2_sb", pos2)]
-        w3_raw = load_words("w3_raw", w3_words)
-        load_scales(w3_plane, w3_scales, (nc.sync,))
 
-        w2_dealt = deal_words("w2_dealt", w2_raw)
+        w2_dealt = deal_words(sb("w2_dealt", [P, 512], I32), w2_raw[:], nc.gpsimd.tensor_copy)
         e_picked_scales = gather_scales("e_picked_scales", e_plane, attr_sb)
         e_picked = gather_words("e_picked", e_table, attr_sb)
-        w2_dealt_scales = deal_scales("w2_dealt_scales", w2_plane, ((0, 2), (2, 4)))
+        w2_dealt_scales = deal_scales(sb("w2_dealt_scales", [P, 512], U8), w2_plane, ((0, 2), (2, 4)), nc.gpsimd)
         r_banks = [
             project("r_bank", t, w2_dealt, w2_dealt_scales[W2_FIRST:, :], e_picked, e_picked_scales[:])
             for t in range(PACK)
         ]
-        x_picked_scales = gather_scales("x_picked_scales", x_plane, offs_sb)
+        x_picked_rows = gather_scales("x_picked_rows", x_plane, offs_sb)
+        for q in range(4):
+            nc.sync.dma_start(
+                x_picked_scales[32 * q + X_FIRST : 32 * q + X_FIRST + 4, :].bitcast(I32),
+                x_picked_rows[4 * q : 4 * q + 4, :].bitcast(I32),
+            )
+        places = [load_list("pos1_sb", pos1), load_list("pos2_sb", pos2)]
+        w3_raw = load_words("w3_raw", w3_words)
+        load_scales(w3_plane, w3_scales, (nc.sync,))
         x_picked = gather_words("x_picked", x_table, offs_sb)
 
         def shared(name, shape, dtype, offset):
@@ -141,11 +144,10 @@ def tile_picked_zcomp_mul_po_kernel(
                 w1_raw[u][:, :, lo - first : hi - first].rearrange("p j (m t) -> p m t j", t=PACK),
             )
 
-        round_w1(nc.gpsimd.tensor_copy, 0, 0, 160)
-        round_w1(nc.vector.tensor_copy, 0, 160, 320)
+        round_w1(nc.vector.tensor_copy, 0, 0, 320)
         round_w1(nc.vector.tensor_copy, 1, 320, 512)
         w1_flat = w1_bf[:].rearrange("p t m j -> p (t m j)")
-        w1_words = [shared("w1_words0", [P, P], U32, 4096), sb("w1_words1", [P, 3 * P], U32)]
+        w1_words = [shared("w1_words0", [P, P], U32, 4096), shared("w1_words1", [P, 3 * P], U32, 20480)]
         w1_scales = [sb("w1_scales0", [P, P], U8), sb("w1_scales1", [P, 3 * P], U8)]
         nc.vector.quantize_mx(out=w1_words[0][:].bitcast(FP8X4), scales=w1_scales[0][:], in_=w1_flat[:, :512])
         nc.vector.quantize_mx(out=w1_words[1][:].bitcast(FP8X4), scales=w1_scales[1][:], in_=w1_flat[:, 512:])
@@ -161,8 +163,6 @@ def tile_picked_zcomp_mul_po_kernel(
         h_banks = [None] + [
             project("h_bank", t, w1_words[1], w1_scales[1][:], x_picked, x_picked_scales[X_FIRST:, :]) for t in range(PACK - 1)
         ]
-        w3_dealt = deal_words("w3_dealt", w3_raw)
-        w3_dealt_scales = deal_scales("w3_dealt_scales", w3_plane, ((0, 4),))
 
         def fetch(name, copy, bank):
             row = sb(name, [P, PICKED], F32)
@@ -174,22 +174,25 @@ def tile_picked_zcomp_mul_po_kernel(
         r_rows = [fetch("r" + str(t), nc.scalar.copy, r_banks[t]) for t in range(PACK)]
         h_rows = [None] * PACK
 
-        def gather_edges_scalar(t, d, offset):
-            picked_edges[t][d] = shared("picked_edges%d_%d" % (t, d), [P, TARGETS], F32, offset)
-            nc.scalar.activation(picked_edges[t][d][:], r_rows[t][:].indirect(edges[d][:]), COPY)
+        def edge_room(t, d, lo, hi):
+            offset = ((8192, 9216), (1024, 4096))[t % 2][d]
+            picked_edges[t][d] = (lo, shared("picked_edges%d_%d_%d" % (t, d, lo), [P, hi - lo], F32, offset))
+            return picked_edges[t][d][1][:], r_rows[t][:].indirect(edges[d][:, lo // 16 : hi // 16])
 
-        def gather_edges_vector(t, d, offset):
-            picked_edges[t][d] = shared("picked_edges%d_%d" % (t, d), [P, TARGETS], F32, offset)
-            nc.vector.tensor_copy(picked_edges[t][d][:], r_rows[t][:].indirect(edges[d][:]))
+        def gather_edges(t, lo, hi, sides=range(2)):
+            for d in sides:
+                nc.scalar.activation(*edge_room(t, d, lo, hi), COPY)
 
         def fetch_nodes(t):
-            h_rows[t] = fetch("h" + str(t), nc.scalar.copy, h_banks[t])
+            h_rows[t] = shared("h" + str(t), [P, PICKED], F32, 10240 + 2048 * t)
+            nc.scalar.copy(h_rows[t][:], h_banks[t][:])
 
         def multiply(t, lo, hi, sides=range(2)):
             for d in sides:
+                first, room = picked_edges[t][d]
                 nc.vector.tensor_tensor(
                     messages[d][:, t, lo:hi], h_rows[t][:].indirect(places[d][:, lo // 16 : hi // 16]),
-                    picked_edges[t][d][:, lo:hi], MULT,
+                    room[:, lo - first : hi - first], MULT,
                 )
 
         pieces = ((0, 128), (128, 192), (192, 256))
@@ -212,27 +215,31 @@ def tile_picked_zcomp_mul_po_kernel(
                 ADD,
             )
 
-        def last_product(k):
+        def last_product(k, split):
             lo, hi = pieces[k]
             nc.vector.quantize_mx(out=z_words[k][:].bitcast(FP8X4), scales=z_scales[k][:], in_=z_bf[k][:])
-            banks = [psum.tile([P, 2, hi - lo], F32, name="y_bank", tag="bank", bufs=8) for pair in range(2)]
+            per_bank = PACK // split
+            banks = [psum.tile([P, per_bank, hi - lo], F32, name="y_bank", tag="bank", bufs=8) for part in range(split)]
             for t in range(PACK):
                 cols = slice(t * P, (t + 1) * P)
                 nc.tensor.matmul_mx(
-                    out=banks[t // 2][:, t % 2, :], lhsT=w3_dealt[:, cols].bitcast(FP8X4), lhsT_scale=w3_dealt_scales[:, cols],
+                    out=banks[t // per_bank][:, t % per_bank, :], lhsT=w3_dealt[:, cols].bitcast(FP8X4),
+                    lhsT_scale=w3_dealt_scales[:, cols],
                     rhs=z_words[k][:].bitcast(FP8X4), rhs_scale=z_scales[k][:], start=True, stop=True,
                 )
             return banks
 
         def fetch_result(k, banks, queue):
             lo, hi = pieces[k]
-            for pair in range(2):
-                nc.scalar.copy(y_f32[k][:, 2 * pair : 2 * pair + 2, :], banks[pair][:])
+            per_bank = PACK // len(banks)
+            for part, bank in enumerate(banks):
+                nc.scalar.copy(y_f32[k][:, per_bank * part : per_bank * (part + 1), :], bank[:])
             queue.dma_start(out_rows[:, :, lo:hi], y_f32[k][:])
 
         def round_result(k, banks, copy):
-            for pair in range(2):
-                copy(y_bf[k][:, :, 2 * pair : 2 * pair + 2], banks[pair][:].rearrange("p t v -> p v t"))
+            per_bank = PACK // len(banks)
+            for part, bank in enumerate(banks):
+                copy(y_bf[k][:, :, per_bank * part : per_bank * (part + 1)], bank[:].rearrange("p t v -> p v t"))
 
         def quantize_result(k):
             lo, hi = pieces[k]
@@ -240,33 +247,37 @@ def tile_picked_zcomp_mul_po_kernel(
                 out=y_words[:, lo:hi].bitcast(FP8X4), scales=y_scales[:, lo:hi], in_=y_bf[k][:].rearrange("p v t -> p (v t)")
             )
 
-        gather_edges_scalar(0, 0, 8192)
-        gather_edges_scalar(0, 1, 9216)
-        gather_edges_vector(1, 0, 1024)
-        h_rows[0] = sb("h0", [P, PICKED], F32)
+        gather_edges(0, 0, TARGETS)
+        nc.vector.tensor_copy(*edge_room(1, 0, 0, TARGETS))
+        h_rows[0] = shared("h0", [P, PICKED], F32, 10240)
         for half in range(2):
             nc.scalar.copy(h_rows[0][:, half * 256 : (half + 1) * 256], first_halves[half][:])
         fetch_nodes(1)
-        gather_edges_scalar(1, 1, 4096)
+        gather_edges(1, 0, TARGETS, (1,))
         multiply(0, 0, TARGETS)
-        gather_edges_scalar(2, 0, 8192)
+        gather_edges(2, 0, 128)
         fetch_nodes(2)
-        gather_edges_scalar(2, 1, 9216)
         multiply(1, 0, TARGETS)
-        gather_edges_scalar(3, 0, 1024)
+        gather_edges(3, 0, 128)
         fetch_nodes(3)
-        gather_edges_scalar(3, 1, 4096)
-        multiply(2, 0, TARGETS)
-        multiply(3, *pieces[0])
-        multiply(3, *pieces[1])
+        multiply(2, 0, 128)
+        w3_dealt_scales = deal_scales(shared("w3_dealt_scales", [P, 512], U8, 12288), w3_plane, ((0, 4),), nc.vector)
+        gather_edges(2, 128, 256)
+        w3_dealt = deal_words(shared("w3_dealt", [P, 512], U32, 20480), w3_raw[:].bitcast(U32), nc.scalar.copy)
+        multiply(3, 0, 128)
+        gather_edges(3, 128, 256)
         add_messages(0)
+        multiply(2, 128, 256, (0,))
+        banks0 = last_product(0, 1)
+        multiply(2, 128, 256, (1,))
+        multiply(3, *pieces[1])
         add_messages(1)
-        banks0 = last_product(0)
-        multiply(3, *pieces[2])
-        banks1 = last_product(1)
+        multiply(3, *pieces[2], (0,))
+        banks1 = last_product(1, 1)
+        multiply(3, *pieces[2], (1,))
         add_messages(2)
-        banks2 = last_product(2)
-        fetch_result(0, banks0, nc.scalar)
+        banks2 = last_product(2, 2)
+        fetch_result(0, banks0, nc.sync)
         round_result(0, banks0, nc.scalar.copy)
         fetch_result(1, banks1, nc.sync)
         round_result(1, banks1, nc.vector.tensor_copy)

@@ -56,6 +56,12 @@ def tile_picked_zcomp_mul_po_kernel(
                 rows = slice(32 * q + first, 32 * q + first + 4)
                 queues[q % len(queues)].dma_start(tile[rows, :].bitcast(I32), src[0, 4 * q : 4 * q + 4, :].bitcast(I32))
 
+        def spread_rows(plane, rows, first):
+            for q in range(4):
+                nc.sync.dma_start(
+                    plane[32 * q + first : 32 * q + first + 4, :].bitcast(I32), rows[4 * q : 4 * q + 4, :].bitcast(I32)
+                )
+
         def deal_words(dealt, words, copy):
             copy(
                 dealt[:].rearrange("p (t c i) -> p c t i", t=PACK, i=4),
@@ -76,8 +82,8 @@ def tile_picked_zcomp_mul_po_kernel(
             nc.vector.tensor_copy(picked[:], words[:].bitcast(U32).indirect(offsets[:]))
             return picked
 
-        def gather_scales(name, scales, offsets):
-            picked = sb(name, [P, PICKED], U8)
+        def gather_scales(name, scales, offsets, tag=None):
+            picked = sb(name, [P, PICKED], U8, tag)
             nc.vector.tensor_copy(picked[:], scales[:].indirect(offsets[:]))
             return picked
 
@@ -95,15 +101,18 @@ def tile_picked_zcomp_mul_po_kernel(
         w2_plane = cleared_plane("w2_plane", 512)
         w3_plane = cleared_plane("w3_plane", 512)
         x_picked_scales = cleared_plane("x_picked_scales", PICKED)
+        w3_dealt_scales = cleared_plane("w3_dealt_scales", 512)
+        nc.gpsimd.dma_start(x_plane[:16, :].bitcast(I32), x_scales[0].bitcast(I32))
+        nc.gpsimd.dma_start(w3_plane[:16, :].bitcast(I32), w3_scales[0].bitcast(I32))
 
         w2_raw = load_words("w2_raw", w2_words)
         attr_sb = load_list("attr_sb", attr)
-        offs_sb = load_list("offs_sb", offs)
         load_scales(e_plane, e_scales, (nc.scalar, nc.sync))
         e_table = load_words("e_table", e_words)
         load_scales(w2_plane, w2_scales, (nc.sync,), range(4), W2_FIRST)
-        nc.sync.dma_start(x_plane[:16, :].bitcast(I32), x_scales[0].bitcast(I32))
+        offs_sb = load_list("offs_sb", offs)
         x_table = load_words("x_table", x_words)
+        edges = [load_list("edge1_sb", edge1)]
         w1_rows = w1.rearrange("(p j) c -> p j c", j=PACK)
         w1_cuts = ((0, 320), (320, 512))
         w1_raw = []
@@ -111,25 +120,33 @@ def tile_picked_zcomp_mul_po_kernel(
             part = sb("w1_raw" + str(u), [P, PACK, hi - lo], F32)
             nc.sync.dma_start(part[:], w1_rows[:, :, lo:hi])
             w1_raw.append(part)
-        edges = [load_list("edge1_sb", edge1), load_list("edge2_sb", edge2)]
+        edges.append(load_list("edge2_sb", edge2))
 
         w2_dealt = deal_words(sb("w2_dealt", [P, 512], I32), w2_raw[:], nc.gpsimd.tensor_copy)
         e_picked_scales = gather_scales("e_picked_scales", e_plane, attr_sb)
-        e_picked = gather_words("e_picked", e_table, attr_sb)
+        e_picked = []
+        for half in range(2):
+            picked = sb("e_picked" + str(half), [P, 256], U32)
+            nc.vector.tensor_copy(picked[:], e_table[:].bitcast(U32).indirect(attr_sb[:, 16 * half : 16 * (half + 1)]))
+            e_picked.append(picked)
         w2_dealt_scales = deal_scales(sb("w2_dealt_scales", [P, 512], U8), w2_plane, ((0, 2), (2, 4)), nc.gpsimd)
-        r_banks = [
-            project("r_bank", t, w2_dealt, w2_dealt_scales[W2_FIRST:, :], e_picked, e_picked_scales[:])
-            for t in range(PACK)
-        ]
+        r_rows = [sb("r" + str(t), [P, PICKED], F32) for t in range(PACK)]
+        for half in range(2):
+            entries = slice(256 * half, 256 * (half + 1))
+            for t in range(PACK):
+                cols = slice(t * P, (t + 1) * P)
+                bank = psum.tile([P, 256], F32, name="r_half", tag="bank", bufs=8)
+                nc.tensor.matmul_mx(
+                    out=bank[:], lhsT=w2_dealt[:, cols].bitcast(FP8X4), lhsT_scale=w2_dealt_scales[W2_FIRST:, cols],
+                    rhs=e_picked[half][:].bitcast(FP8X4), rhs_scale=e_picked_scales[:, entries], start=True, stop=True,
+                )
+                nc.scalar.copy(r_rows[t][:, entries], bank[:])
         x_picked_rows = gather_scales("x_picked_rows", x_plane, offs_sb)
-        for q in range(4):
-            nc.sync.dma_start(
-                x_picked_scales[32 * q + X_FIRST : 32 * q + X_FIRST + 4, :].bitcast(I32),
-                x_picked_rows[4 * q : 4 * q + 4, :].bitcast(I32),
-            )
+        spread_rows(x_picked_scales, x_picked_rows, X_FIRST)
         places = [load_list("pos1_sb", pos1), load_list("pos2_sb", pos2)]
         w3_raw = load_words("w3_raw", w3_words)
-        load_scales(w3_plane, w3_scales, (nc.sync,))
+        w3_dealt_rows = deal_scales(sb("w3_dealt_rows", [P, 512], U8, "w2_plane"), w3_plane, ((0, 4),), nc.gpsimd)
+        spread_rows(w3_dealt_scales, w3_dealt_rows, 0)
         x_picked = gather_words("x_picked", x_table, offs_sb)
 
         def shared(name, shape, dtype, offset):
@@ -147,7 +164,7 @@ def tile_picked_zcomp_mul_po_kernel(
         round_w1(nc.vector.tensor_copy, 0, 0, 320)
         round_w1(nc.vector.tensor_copy, 1, 320, 512)
         w1_flat = w1_bf[:].rearrange("p t m j -> p (t m j)")
-        w1_words = [shared("w1_words0", [P, P], U32, 4096), shared("w1_words1", [P, 3 * P], U32, 20480)]
+        w1_words = [shared("w1_words0", [P, P], U32, 4096), sb("w1_words1", [P, 3 * P], U32)]
         w1_scales = [sb("w1_scales0", [P, P], U8), sb("w1_scales1", [P, 3 * P], U8)]
         nc.vector.quantize_mx(out=w1_words[0][:].bitcast(FP8X4), scales=w1_scales[0][:], in_=w1_flat[:, :512])
         nc.vector.quantize_mx(out=w1_words[1][:].bitcast(FP8X4), scales=w1_scales[1][:], in_=w1_flat[:, 512:])
@@ -164,18 +181,12 @@ def tile_picked_zcomp_mul_po_kernel(
             project("h_bank", t, w1_words[1], w1_scales[1][:], x_picked, x_picked_scales[X_FIRST:, :]) for t in range(PACK - 1)
         ]
 
-        def fetch(name, copy, bank):
-            row = sb(name, [P, PICKED], F32)
-            copy(row[:], bank[:])
-            return row
-
         picked_edges = [[None, None] for t in range(PACK)]
         messages = [sb("messages" + str(d), [P, PACK, TARGETS], F32) for d in range(2)]
-        r_rows = [fetch("r" + str(t), nc.scalar.copy, r_banks[t]) for t in range(PACK)]
         h_rows = [None] * PACK
 
         def edge_room(t, d, lo, hi):
-            offset = ((8192, 9216), (1024, 4096))[t % 2][d]
+            offset = ((8192, 3072), (9216, 4096))[t % 2][d] + 2 * lo
             picked_edges[t][d] = (lo, shared("picked_edges%d_%d_%d" % (t, d, lo), [P, hi - lo], F32, offset))
             return picked_edges[t][d][1][:], r_rows[t][:].indirect(edges[d][:, lo // 16 : hi // 16])
 
@@ -247,8 +258,9 @@ def tile_picked_zcomp_mul_po_kernel(
                 out=y_words[:, lo:hi].bitcast(FP8X4), scales=y_scales[:, lo:hi], in_=y_bf[k][:].rearrange("p v t -> p (v t)")
             )
 
-        gather_edges(0, 0, TARGETS)
-        nc.vector.tensor_copy(*edge_room(1, 0, 0, TARGETS))
+        gather_edges(0, 0, TARGETS, (0,))
+        gather_edges(1, 0, TARGETS, (0,))
+        nc.vector.tensor_copy(*edge_room(0, 1, 0, TARGETS))
         h_rows[0] = shared("h0", [P, PICKED], F32, 10240)
         for half in range(2):
             nc.scalar.copy(h_rows[0][:, half * 256 : (half + 1) * 256], first_halves[half][:])
@@ -257,13 +269,12 @@ def tile_picked_zcomp_mul_po_kernel(
         multiply(0, 0, TARGETS)
         gather_edges(2, 0, 128)
         fetch_nodes(2)
+        fetch_nodes(3)
         multiply(1, 0, TARGETS)
         gather_edges(3, 0, 128)
-        fetch_nodes(3)
         multiply(2, 0, 128)
-        w3_dealt_scales = deal_scales(shared("w3_dealt_scales", [P, 512], U8, 12288), w3_plane, ((0, 4),), nc.vector)
         gather_edges(2, 128, 256)
-        w3_dealt = deal_words(shared("w3_dealt", [P, 512], U32, 20480), w3_raw[:].bitcast(U32), nc.scalar.copy)
+        w3_dealt = deal_words(shared("w3_dealt", [P, 512], U32, 1280), w3_raw[:].bitcast(U32), nc.scalar.copy)
         multiply(3, 0, 128)
         gather_edges(3, 128, 256)
         add_messages(0)
@@ -285,7 +296,8 @@ def tile_picked_zcomp_mul_po_kernel(
         quantize_result(1)
         nc.sync.dma_start(out_words[:, :192], y_words[:, :192])
         fetch_result(2, banks2, nc.sync)
-        round_result(2, banks2, nc.vector.tensor_copy)
+        for pair, copy in enumerate((nc.vector.tensor_copy, nc.scalar.copy)):
+            copy(y_bf[2][:, :, 2 * pair : 2 * pair + 2], banks2[pair][:].rearrange("p t v -> p v t"))
         quantize_result(2)
         nc.scalar.dma_start(out_words[:, 192:], y_words[:, 192:])
         for q in range(4):

@@ -101,16 +101,14 @@ def tile_picked_zcomp_mul_po_kernel(
         w2_plane = cleared_plane("w2_plane", 512)
         w3_plane = cleared_plane("w3_plane", 512)
         x_picked_scales = cleared_plane("x_picked_scales", PICKED)
-        w3_dealt_scales = cleared_plane("w3_dealt_scales", 512)
-        nc.gpsimd.dma_start(x_plane[:16, :].bitcast(I32), x_scales[0].bitcast(I32))
-        nc.gpsimd.dma_start(w3_plane[:16, :].bitcast(I32), w3_scales[0].bitcast(I32))
 
         w2_raw = load_words("w2_raw", w2_words)
         attr_sb = load_list("attr_sb", attr)
+        offs_sb = load_list("offs_sb", offs)
         load_scales(e_plane, e_scales, (nc.scalar, nc.sync))
         e_table = load_words("e_table", e_words)
         load_scales(w2_plane, w2_scales, (nc.sync,), range(4), W2_FIRST)
-        offs_sb = load_list("offs_sb", offs)
+        nc.sync.dma_start(x_plane[:16, :].bitcast(I32), x_scales[0].bitcast(I32))
         x_table = load_words("x_table", x_words)
         edges = [load_list("edge1_sb", edge1)]
         w1_rows = w1.rearrange("(p j) c -> p j c", j=PACK)
@@ -122,31 +120,24 @@ def tile_picked_zcomp_mul_po_kernel(
             w1_raw.append(part)
         edges.append(load_list("edge2_sb", edge2))
 
-        w2_dealt = deal_words(sb("w2_dealt", [P, 512], I32), w2_raw[:], nc.gpsimd.tensor_copy)
+        w2_dealt = deal_words(sb("w2_dealt", [P, 512], U32), w2_raw[:].bitcast(U32), nc.scalar.copy)
         e_picked_scales = gather_scales("e_picked_scales", e_plane, attr_sb)
-        e_picked = []
-        for half in range(2):
-            picked = sb("e_picked" + str(half), [P, 256], U32)
-            nc.vector.tensor_copy(picked[:], e_table[:].bitcast(U32).indirect(attr_sb[:, 16 * half : 16 * (half + 1)]))
-            e_picked.append(picked)
-        w2_dealt_scales = deal_scales(sb("w2_dealt_scales", [P, 512], U8), w2_plane, ((0, 2), (2, 4)), nc.gpsimd)
+        e_picked = gather_words("e_picked", e_table, attr_sb)
+        w2_dealt_scales = deal_scales(sb("w2_dealt_scales", [P, 512], U8), w2_plane, ((0, 1), (1, 2), (2, 3), (3, 4)), nc.gpsimd)
         r_rows = [sb("r" + str(t), [P, PICKED], F32) for t in range(PACK)]
-        for half in range(2):
-            entries = slice(256 * half, 256 * (half + 1))
-            for t in range(PACK):
-                cols = slice(t * P, (t + 1) * P)
-                bank = psum.tile([P, 256], F32, name="r_half", tag="bank", bufs=8)
-                nc.tensor.matmul_mx(
-                    out=bank[:], lhsT=w2_dealt[:, cols].bitcast(FP8X4), lhsT_scale=w2_dealt_scales[W2_FIRST:, cols],
-                    rhs=e_picked[half][:].bitcast(FP8X4), rhs_scale=e_picked_scales[:, entries], start=True, stop=True,
-                )
-                nc.scalar.copy(r_rows[t][:, entries], bank[:])
+        for t, lo, hi in ((0, 0, 256), (0, 256, 512), (1, 0, 512), (2, 0, 512), (3, 0, 512)):
+            cols = slice(t * P, (t + 1) * P)
+            bank = psum.tile([P, hi - lo], F32, name="r_bank", tag="bank", bufs=8)
+            nc.tensor.matmul_mx(
+                out=bank[:], lhsT=w2_dealt[:, cols].bitcast(FP8X4), lhsT_scale=w2_dealt_scales[W2_FIRST:, cols],
+                rhs=e_picked[:, lo:hi].bitcast(FP8X4), rhs_scale=e_picked_scales[:, lo:hi], start=True, stop=True,
+            )
+            nc.scalar.copy(r_rows[t][:, lo:hi], bank[:])
         x_picked_rows = gather_scales("x_picked_rows", x_plane, offs_sb)
         spread_rows(x_picked_scales, x_picked_rows, X_FIRST)
         places = [load_list("pos1_sb", pos1), load_list("pos2_sb", pos2)]
         w3_raw = load_words("w3_raw", w3_words)
-        w3_dealt_rows = deal_scales(sb("w3_dealt_rows", [P, 512], U8, "w2_plane"), w3_plane, ((0, 4),), nc.gpsimd)
-        spread_rows(w3_dealt_scales, w3_dealt_rows, 0)
+        load_scales(w3_plane, w3_scales, (nc.sync,))
         x_picked = gather_words("x_picked", x_table, offs_sb)
 
         def shared(name, shape, dtype, offset):
@@ -273,6 +264,7 @@ def tile_picked_zcomp_mul_po_kernel(
         multiply(1, 0, TARGETS)
         gather_edges(3, 0, 128)
         multiply(2, 0, 128)
+        w3_dealt_scales = deal_scales(shared("w3_dealt_scales", [P, 512], U8, 12288), w3_plane, ((0, 4),), nc.vector)
         gather_edges(2, 128, 256)
         w3_dealt = deal_words(shared("w3_dealt", [P, 512], U32, 1280), w3_raw[:].bitcast(U32), nc.scalar.copy)
         multiply(3, 0, 128)

@@ -148,8 +148,8 @@ def tile_picked_zcomp_mul_po_kernel(
         def round_w1(copy, u, lo, hi):
             first = w1_cuts[u][0]
             copy(
-                w1_bf[:, :, lo // PACK : hi // PACK, :].rearrange("p t m j -> p m t j"),
-                w1_raw[u][:, :, lo - first : hi - first].rearrange("p j (m t) -> p m t j", t=PACK),
+                w1_bf[:, :, lo // PACK : hi // PACK, :].rearrange("p t m j -> p m j t"),
+                w1_raw[u][:, :, lo - first : hi - first].rearrange("p j (m t) -> p m j t", t=PACK),
             )
 
         round_w1(nc.vector.tensor_copy, 0, 0, 320)

@@ -282,16 +282,16 @@ def tile_picked_zcomp_mul_po_kernel(
         banks2 = last_product(2, 2)
         fetch_result(0, banks0, nc.sync)
         round_result(0, banks0, nc.scalar.copy)
+        quantize_result(0)
+        nc.sync.dma_start(out_words[:, :128], y_words[:, :128])
         fetch_result(1, banks1, nc.sync)
         round_result(1, banks1, nc.vector.tensor_copy)
-        quantize_result(0)
         quantize_result(1)
-        nc.sync.dma_start(out_words[:, :192], y_words[:, :192])
         fetch_result(2, banks2, nc.sync)
         for pair, copy in enumerate((nc.vector.tensor_copy, nc.scalar.copy)):
             copy(y_bf[2][:, :, 2 * pair : 2 * pair + 2], banks2[pair][:].rearrange("p t v -> p v t"))
         quantize_result(2)
-        nc.scalar.dma_start(out_words[:, 192:], y_words[:, 192:])
+        nc.scalar.dma_start(out_words[:, 128:], y_words[:, 128:])
         for q in range(4):
             queue = nc.sync if q else nc.scalar
             queue.dma_start(out_2[0, 4 * q : 4 * q + 4, :].bitcast(I32), y_scales[32 * q : 32 * q + 4, :].bitcast(I32))

from contextlib import ExitStack

import concourse.mybir as mybir

F32 = mybir.dt.float32
BF16 = mybir.dt.bfloat16
I32 = mybir.dt.int32
U32 = mybir.dt.uint32
U16 = mybir.dt.uint16
U8 = mybir.dt.uint8
FP8X4 = mybir.dt.float8_e4m3fn_x4
MULT = mybir.AluOpType.mult
ADD = mybir.AluOpType.add
COPY = mybir.ActivationFunctionType.Copy

P = 128
PACK = 4
TABLE = 1024
PICKED = 512
TARGETS = 256
X_FIRST = 4
W2_FIRST = 8
FLOPS = 2 * 512 * 512 * (2 * PICKED + TARGETS)


def tile_picked_zcomp_mul_po_kernel(
    tc, x_words, x_scales, e_words, e_scales, w1, w2_words, w2_scales, w3_words, w3_scales,
    offs, pos1, pos2, attr, edge1, edge2, out_0, out_1, out_2,
):
    nc = tc.nc
    with ExitStack() as ctx:
        pool = ctx.enter_context(tc.tile_pool(name="sbuf", bufs=1))
        reused = ctx.enter_context(tc.tile_pool(name="reused", bufs=1))
        psum = ctx.enter_context(tc.psum_pool(name="psum", bufs=1))

        def sb(name, shape, dtype, tag=None):
            return pool.tile(shape, dtype, name=name, tag=tag or name, align_bytes=64)

        def load_list(name, src):
            tile = pool.tile(list(src.shape), U16, name=name)
            nc.sync.dma_start(tile[:], src)
            return tile

        def load_words(name, src):
            tile = sb(name, [P, src.shape[2]], I32)
            nc.sync.dma_start(tile[:], src[0].rearrange("p n t -> p (n t)").bitcast(I32))
            return tile

        def cleared_plane(name, width):
            tile = sb(name, [P, width], U8)
            nc.vector.memset(tile[:].bitcast(I32), 0)
            return tile

        def load_scales(tile, src, queues, quadrants=range(4), first=0):
            for q in quadrants:
                rows = slice(32 * q + first, 32 * q + first + 4)
                queues[q % len(queues)].dma_start(tile[rows, :].bitcast(I32), src[0, 4 * q : 4 * q + 4, :].bitcast(I32))

        def spread_rows(plane, rows, first):
            for q in range(4):
                nc.sync.dma_start(
                    plane[32 * q + first : 32 * q + first + 4, :].bitcast(I32), rows[4 * q : 4 * q + 4, :].bitcast(I32)
                )

        def deal_words(dealt, words, copy):
            copy(
                dealt[:].rearrange("p (t c i) -> p c t i", t=PACK, i=4),
                words.rearrange("p (c i t) -> p c t i", t=PACK, i=4),
            )
            return dealt

        def deal_scales(dealt, scales, cuts, engine):
            for lo, hi in cuts:
                engine.tensor_copy(
                    dealt[:].rearrange("p (t m) -> p t m", t=PACK)[:, lo:hi, :],
                    scales[:].rearrange("p (m t) -> p t m", t=PACK)[:, lo:hi, :],
                )
            return dealt

        def gather_words(name, words, offsets, tag=None):
            picked = sb(name, [P, PICKED], U32, tag)
            nc.vector.tensor_copy(picked[:], words[:].bitcast(U32).indirect(offsets[:]))
            return picked

        def gather_scales(name, scales, offsets, tag=None):
            picked = sb(name, [P, PICKED], U8, tag)
            nc.vector.tensor_copy(picked[:], scales[:].indirect(offsets[:]))
            return picked

        def project(name, t, w_words, w_scales, words, scales):
            cols = slice(t * P, (t + 1) * P)
            bank = psum.tile([P, PICKED], F32, name=name, tag="bank", bufs=8)
            nc.tensor.matmul_mx(
                out=bank[:], lhsT=w_words[:, cols].bitcast(FP8X4), lhsT_scale=w_scales[:, cols],
                rhs=words[:].bitcast(FP8X4), rhs_scale=scales, start=True, stop=True,
            )
            return bank

        e_plane = cleared_plane("e_plane", TABLE)
        x_plane = cleared_plane("x_plane", TABLE)
        w2_plane = cleared_plane("w2_plane", 512)
        w3_plane = cleared_plane("w3_plane", 512)
        x_picked_scales = cleared_plane("x_picked_scales", PICKED)

        w2_raw = load_words("w2_raw", w2_words)
        attr_sb = load_list("attr_sb", attr)
        offs_sb = load_list("offs_sb", offs)
        load_scales(e_plane, e_scales, (nc.scalar, nc.sync))
        e_table = load_words("e_table", e_words)
        load_scales(w2_plane, w2_scales, (nc.sync,), range(4), W2_FIRST)
        nc.sync.dma_start(x_plane[:16, :].bitcast(I32), x_scales[0].bitcast(I32))
        x_table = load_words("x_table", x_words)
        edges = [load_list("edge1_sb", edge1)]
        w1_rows = w1.rearrange("(p j) c -> p j c", j=PACK)
        w1_cuts = ((0, 320), (320, 512))
        w1_raw = []
        for u, (lo, hi) in enumerate(w1_cuts):
            part = sb("w1_raw" + str(u), [P, PACK, hi - lo], F32)
            nc.sync.dma_start(part[:], w1_rows[:, :, lo:hi])
            w1_raw.append(part)
        edges.append(load_list("edge2_sb", edge2))

        w2_dealt = deal_words(sb("w2_dealt", [P, 512], U32), w2_raw[:].bitcast(U32), nc.scalar.copy)
        e_picked_scales = gather_scales("e_picked_scales", e_plane, attr_sb)
        e_picked = gather_words("e_picked", e_table, attr_sb)
        w2_dealt_scales = deal_scales(sb("w2_dealt_scales", [P, 512], U8), w2_plane, ((0, 1), (1, 2), (2, 3), (3, 4)), nc.gpsimd)
        r_rows = [sb("r" + str(t), [P, PICKED], F32) for t in range(PACK)]
        for t, lo, hi in ((0, 0, 256), (0, 256, 512), (1, 0, 512), (2, 0, 512), (3, 0, 512)):
            cols = slice(t * P, (t + 1) * P)
            bank = psum.tile([P, hi - lo], F32, name="r_bank", tag="bank", bufs=8)
            nc.tensor.matmul_mx(
                out=bank[:], lhsT=w2_dealt[:, cols].bitcast(FP8X4), lhsT_scale=w2_dealt_scales[W2_FIRST:, cols],
                rhs=e_picked[:, lo:hi].bitcast(FP8X4), rhs_scale=e_picked_scales[:, lo:hi], start=True, stop=True,
            )
            nc.scalar.copy(r_rows[t][:, lo:hi], bank[:])
        x_picked_rows = gather_scales("x_picked_rows", x_plane, offs_sb)
        spread_rows(x_picked_scales, x_picked_rows, X_FIRST)
        places = [load_list("pos1_sb", pos1), load_list("pos2_sb", pos2)]
        w3_raw = load_words("w3_raw", w3_words)
        load_scales(w3_plane, w3_scales, (nc.sync,))
        x_picked = gather_words("x_picked", x_table, offs_sb)

        def shared(name, shape, dtype, offset):
            return reused.tile(shape, dtype, name=name, align_bytes=64, offset=offset)

        w1_bf = shared("w1_bf", [P, PACK, P, PACK], BF16, 0)

        def round_w1(copy, u, lo, hi):
            first = w1_cuts[u][0]
            copy(
                w1_bf[:, :, lo // PACK : hi // PACK, :].rearrange("p t m j -> p m j t"),
                w1_raw[u][:, :, lo - first : hi - first].rearrange("p j (m t) -> p m j t", t=PACK),
            )

        round_w1(nc.vector.tensor_copy, 0, 0, 320)
        round_w1(nc.vector.tensor_copy, 1, 320, 512)
        w1_flat = w1_bf[:].rearrange("p t m j -> p (t m j)")
        w1_words = [shared("w1_words0", [P, P], U32, 4096), sb("w1_words1", [P, 3 * P], U32)]
        w1_scales = [sb("w1_scales0", [P, P], U8), sb("w1_scales1", [P, 3 * P], U8)]
        nc.vector.quantize_mx(out=w1_words[0][:].bitcast(FP8X4), scales=w1_scales[0][:], in_=w1_flat[:, :512])
        nc.vector.quantize_mx(out=w1_words[1][:].bitcast(FP8X4), scales=w1_scales[1][:], in_=w1_flat[:, 512:])
        first_halves = []
        for half in range(2):
            cols = slice(half * 256, (half + 1) * 256)
            bank = psum.tile([P, 256], F32, name="h_half", tag="bank", bufs=8)
            nc.tensor.matmul_mx(
                out=bank[:], lhsT=w1_words[0][:].bitcast(FP8X4), lhsT_scale=w1_scales[0][:],
                rhs=x_picked[:, cols].bitcast(FP8X4), rhs_scale=x_picked_scales[X_FIRST:, cols], start=True, stop=True,
            )
            first_halves.append(bank)
        h_banks = [None] + [
            project("h_bank", t, w1_words[1], w1_scales[1][:], x_picked, x_picked_scales[X_FIRST:, :]) for t in range(PACK - 1)
        ]

        picked_edges = [[None, None] for t in range(PACK)]
        messages = [sb("messages" + str(d), [P, PACK, TARGETS], F32) for d in range(2)]
        h_rows = [None] * PACK

        def edge_room(t, d, lo, hi):
            offset = ((8192, 3072), (9216, 4096))[t % 2][d] + 2 * lo
            picked_edges[t][d] = (lo, shared("picked_edges%d_%d_%d" % (t, d, lo), [P, hi - lo], F32, offset))
            return picked_edges[t][d][1][:], r_rows[t][:].indirect(edges[d][:, lo // 16 : hi // 16])

        def gather_edges(t, lo, hi, sides=range(2)):
            for d in sides:
                nc.scalar.activation(*edge_room(t, d, lo, hi), COPY)

        def fetch_nodes(t):
            h_rows[t] = shared("h" + str(t), [P, PICKED], F32, 10240 + 2048 * t)
            nc.scalar.copy(h_rows[t][:], h_banks[t][:])

        def multiply(t, lo, hi, sides=range(2)):
            for d in sides:
                first, room = picked_edges[t][d]
                nc.vector.tensor_tensor(
                    messages[d][:, t, lo:hi], h_rows[t][:].indirect(places[d][:, lo // 16 : hi // 16]),
                    room[:, lo - first : hi - first], MULT,
                )

        pieces = ((0, 128), (128, 192), (192, 256))
        z_bf = [sb("z_bf" + str(k), [P, (hi - lo) * PACK], BF16) for k, (lo, hi) in enumerate(pieces)]
        z_words = [sb("z_words" + str(k), [P, hi - lo], U32) for k, (lo, hi) in enumerate(pieces)]
        z_scales = [sb("z_scales" + str(k), [P, hi - lo], U8) for k, (lo, hi) in enumerate(pieces)]
        y_f32 = [sb("y_f32" + str(k), [P, PACK, hi - lo], F32) for k, (lo, hi) in enumerate(pieces)]
        y_bf = [sb("y_bf" + str(k), [P, hi - lo, PACK], BF16) for k, (lo, hi) in enumerate(pieces)]
        y_words = sb("y_words", [P, TARGETS], I32)
        y_scales = sb("y_scales", [P, TARGETS], U8)
        out_rows = out_0.rearrange("(p t) v -> p t v", t=PACK)
        out_words = out_1[0].rearrange("p v t -> p (v t)").bitcast(I32)

        def add_messages(k):
            lo, hi = pieces[k]
            nc.vector.tensor_tensor(
                z_bf[k][:].rearrange("p (c i t) -> p c t i", t=PACK, i=4),
                messages[0][:, :, lo:hi].rearrange("p t (c i) -> p c t i", i=4),
                messages[1][:, :, lo:hi].rearrange("p t (c i) -> p c t i", i=4),
                ADD,
            )

        def last_product(k, split):
            lo, hi = pieces[k]
            nc.vector.quantize_mx(out=z_words[k][:].bitcast(FP8X4), scales=z_scales[k][:], in_=z_bf[k][:])
            per_bank = PACK // split
            banks = [psum.tile([P, per_bank, hi - lo], F32, name="y_bank", tag="bank", bufs=8) for part in range(split)]
            for t in range(PACK):
                cols = slice(t * P, (t + 1) * P)
                nc.tensor.matmul_mx(
                    out=banks[t // per_bank][:, t % per_bank, :], lhsT=w3_dealt[:, cols].bitcast(FP8X4),
                    lhsT_scale=w3_dealt_scales[:, cols],
                    rhs=z_words[k][:].bitcast(FP8X4), rhs_scale=z_scales[k][:], start=True, stop=True,
                )
            return banks

        def fetch_result(k, banks, queue):
            lo, hi = pieces[k]
            per_bank = PACK // len(banks)
            for part, bank in enumerate(banks):
                nc.scalar.copy(y_f32[k][:, per_bank * part : per_bank * (part + 1), :], bank[:])
            queue.dma_start(out_rows[:, :, lo:hi], y_f32[k][:])

        def round_result(k, banks, copy):
            per_bank = PACK // len(banks)
            for part, bank in enumerate(banks):
                copy(y_bf[k][:, :, per_bank * part : per_bank * (part + 1)], bank[:].rearrange("p t v -> p v t"))

        def quantize_result(k):
            lo, hi = pieces[k]
            nc.vector.quantize_mx(
                out=y_words[:, lo:hi].bitcast(FP8X4), scales=y_scales[:, lo:hi], in_=y_bf[k][:].rearrange("p v t -> p (v t)")
            )

        gather_edges(0, 0, TARGETS, (0,))
        gather_edges(1, 0, TARGETS, (0,))
        nc.vector.tensor_copy(*edge_room(0, 1, 0, TARGETS))
        h_rows[0] = shared("h0", [P, PICKED], F32, 10240)
        for half in range(2):
            nc.scalar.copy(h_rows[0][:, half * 256 : (half + 1) * 256], first_halves[half][:])
        fetch_nodes(1)
        gather_edges(1, 0, TARGETS, (1,))
        multiply(0, 0, TARGETS)
        gather_edges(2, 0, 128)
        fetch_nodes(2)
        fetch_nodes(3)
        multiply(1, 0, TARGETS)
        gather_edges(3, 0, 128)
        multiply(2, 0, 128)
        w3_dealt_scales = deal_scales(shared("w3_dealt_scales", [P, 512], U8, 12288), w3_plane, ((0, 4),), nc.vector)
        gather_edges(2, 128, 256)
        w3_dealt = deal_words(shared("w3_dealt", [P, 512], U32, 1280), w3_raw[:].bitcast(U32), nc.scalar.copy)
        multiply(3, 0, 128)
        gather_edges(3, 128, 256)
        add_messages(0)
        multiply(2, 128, 256, (0,))
        banks0 = last_product(0, 1)
        multiply(2, 128, 256, (1,))
        multiply(3, *pieces[1])
        add_messages(1)
        multiply(3, *pieces[2], (0,))
        banks1 = last_product(1, 1)
        multiply(3, *pieces[2], (1,))
        add_messages(2)
        banks2 = last_product(2, 2)
        fetch_result(0, banks0, nc.sync)
        round_result(0, banks0, nc.scalar.copy)
        quantize_result(0)
        nc.sync.dma_start(out_words[:, :128], y_words[:, :128])
        fetch_result(1, banks1, nc.sync)
        round_result(1, banks1, nc.vector.tensor_copy)
        quantize_result(1)
        fetch_result(2, banks2, nc.sync)
        for pair, copy in enumerate((nc.vector.tensor_copy, nc.scalar.copy)):
            copy(y_bf[2][:, :, 2 * pair : 2 * pair + 2], banks2[pair][:].rearrange("p t v -> p v t"))
        quantize_result(2)
        nc.scalar.dma_start(out_words[:, 128:], y_words[:, 128:])
        for q in range(4):
            queue = nc.sync if q else nc.scalar
            queue.dma_start(out_2[0, 4 * q : 4 * q + 4, :].bitcast(I32), y_scales[32 * q : 32 * q + 4, :].bitcast(I32))
